import numpy as np
import ml_dtypes


def mxq(x, axis, fmt="e4m3"):
    dtype, down = {"e4m3": (ml_dtypes.float8_e4m3fn, 7), "e5m2": (ml_dtypes.float8_e5m2, 14)}[fmt]
    v = np.moveaxis(np.asarray(x, np.float32).astype(ml_dtypes.bfloat16).astype(np.float64), axis, -1)
    blocks = v.reshape(v.shape[:-1] + (-1, 32))
    amax = np.abs(blocks).max(-1, keepdims=True)
    byte = np.maximum(np.where(amax > 0, np.frexp(amax)[1] - 1 + 127, 0) - down, 1)
    scale = np.exp2(byte - 127.0)
    codes = (blocks / scale).astype(np.float32).astype(dtype).astype(np.float64)
    return np.moveaxis((codes * scale).reshape(v.shape), -1, axis)


WIDE = False


def mx_kscale(k):
    if not WIDE:
        return np.ones(k)
    levels = np.array([18, -18])
    if k % 512:
        return np.exp2(np.random.permutation(np.resize(levels, k // 32))).repeat(32)
    a = np.empty((k // 512, 16))
    for p in range(k // 512):
        a[p, :8] = np.random.permutation(np.resize(levels, 8))
        for g in range(8):
            far = levels[np.abs(levels - a[p, g]) >= 10]
            a[p, g + 8] = far[np.random.randint(len(far))]
    return np.exp2(a.ravel()).repeat(32)


def f64(x):
    return np.asarray(x).astype(np.float64)


def striped(idx):
    return np.tile(np.asarray(idx).reshape(-1, 16).T, (8, 1)).astype(np.uint16)


def unstriped(offs):
    return offs[:16].T.reshape(-1).astype(np.int64)


E2M1 = np.array([0.0, 0.5, 1.0, 1.5, 2.0, 3.0, 4.0, 6.0, -0.0, -0.5, -1.0, -1.5, -2.0, -3.0, -4.0, -6.0])


def pack_weight(w, fmt):
    k, n = w.shape
    w = f64(np.asarray(w, np.float32).astype(ml_dtypes.bfloat16)).reshape(k // 32, 32, n)
    amax = np.abs(w).max(1)
    if fmt == "e4m3":
        byte = np.frexp(amax)[1] - 1 + 127 - 7
    else:
        mant, ex = np.frexp(amax / 6.0)
        byte = np.where(mant > 0.5, ex, ex - 1) + 127
    byte = np.clip(np.where(amax > 0, byte, 1), 1, 254)
    scaled = (w * np.exp2(127.0 - byte)[:, None, :]).reshape(k, n).astype(np.float32)
    by_word = np.ascontiguousarray(scaled.reshape(k // 512, 128, 4, n).transpose(0, 1, 3, 2))
    if fmt == "e4m3":
        words = by_word.astype(ml_dtypes.float8_e4m3fn).view(np.uint8)
    else:
        c = by_word.astype(ml_dtypes.float4_e2m1fn).view(np.uint8) & 0xF
        words = (c[..., 0::2] | (c[..., 1::2] << 4)).reshape(k // 512, 128, 2 * n)
    return np.ascontiguousarray(words), np.ascontiguousarray(byte.astype(np.uint8).reshape(k // 512, 16, n))


def unpack_weight(words, scales, fmt):
    g, _, n = scales.shape
    words = np.ascontiguousarray(words).reshape(g, 128, n, -1)
    if fmt == "e4m3":
        vals = words.view(ml_dtypes.float8_e4m3fn).astype(np.float64)
    else:
        nib = np.empty((g, 128, n, 4), np.uint8)
        nib[..., 0::2] = words & 0xF
        nib[..., 1::2] = words >> 4
        vals = E2M1[nib]
    vals = vals * np.repeat(np.exp2(scales.astype(np.float64) - 127.0), 8, axis=1)[..., None]
    return vals.transpose(0, 1, 3, 2).reshape(g * 512, n)


N, T, D, V = 512, 2048, 1024, 512


def setup_inputs():
    n = np.random.standard_normal
    idx = np.random.permutation(T)[:N]
    s = mx_kscale(D)[:, None]
    z = mx_kscale(V)[:, None]
    w = n((D, V)) / np.sqrt(D)
    wd, wv = pack_weight(w * s, "e4m3"), pack_weight(w.T / z, "e4m3")
    return {
        "xT": (n((D, T)) / s).astype(np.float32),
        "wd_words": wd[0],
        "wd_scales": wd[1],
        "wv_words": wv[0],
        "wv_scales": wv[1],
        "y": n((V, N)).astype(np.float32),
        "cw": (np.random.uniform(0.5, 1.5, (V, 1)) / np.sqrt(V) * z).astype(np.float32),
        "rw": np.tile(np.random.uniform(0.5, 1.5, N), (128, 1)).astype(np.float32),
        "offs": striped(idx),
    }


def reference(xT, wd_words, wd_scales, wv_words, wv_scales, y, cw, rw, offs):
    idx = unstriped(offs)
    a = unpack_weight(wd_words, wd_scales, "e4m3").T @ mxq(f64(xT)[:, idx], 0, "e4m3")
    g = f64(cw) * f64(rw)[:1] * np.minimum(np.maximum(a - f64(y), -1.0), 1.0)
    dx = unpack_weight(wv_words, wv_scales, "e4m3").T @ mxq(g, 0, "e5m2")
    gx = np.zeros((D, T))
    gx[:, idx] = dx
    return gx

@@ -1,0 +1,179 @@
+from contextlib import ExitStack
+
+import concourse.mybir as mybir
+
+N, T, D, V = 512, 2048, 1024, 512
+FLOPS = 2 * 2 * N * D * V
+
+F32 = mybir.dt.float32
+BF16 = mybir.dt.bfloat16
+I32 = mybir.dt.int32
+U32 = mybir.dt.uint32
+U16 = mybir.dt.uint16
+U8 = mybir.dt.uint8
+E4M3X4 = mybir.dt.float8_e4m3fn_x4
+E5M2X4 = mybir.dt.float8_e5m2_x4
+ALU = mybir.AluOpType
+COPY = mybir.ActivationFunctionType.Copy
+
+P = 128
+PACK = 4
+K_PASS = P * PACK
+PASSES = D // K_PASS
+HALVES = 2
+H = N // HALVES
+D_TILES = D // P
+WINDOWS = 3
+
+
+def tile_attend_gml_hub_kernel(tc, xT, wd_words, wd_scales, wv_words, wv_scales, y, cw, rw, offs, out):
+    nc = tc.nc
+    with ExitStack() as ctx:
+        keep = ctx.enter_context(tc.tile_pool(name="keep", bufs=1))
+        psum = ctx.enter_context(tc.psum_pool(name="psum", bufs=1))
+
+        def sb(name, shape, dtype):
+            return keep.tile(shape, dtype, name=name, align_bytes=64)
+
+        offsets = keep.tile([P, N // 16], U16, name="offsets")
+        nc.sync.dma_start(offsets[:], offs)
+
+        wd_sc_raw = sb("wd_sc_raw", [P, V], U8)
+        wv_sc = sb("wv_sc", [P, D], U8)
+        nc.gpsimd.memset(wd_sc_raw[:].bitcast(I32), 0)
+        nc.gpsimd.memset(wv_sc[:].bitcast(I32), 0)
+        windows = [sb(f"window{w}", [P, T], F32) for w in range(WINDOWS)]
+        for w in range(WINDOWS):
+            nc.vector.memset(windows[w][:], 0.0)
+
+        x_planes = xT.rearrange("(o p t) n -> o t p n", o=PASSES, t=PACK)
+        x_sb = [[sb(f"x{o}_{t}", [P, T], F32) for t in range(PACK)] for o in range(PASSES)]
+
+        def load_x(o, t):
+            nc.sync.dma_start(x_sb[o][t][:], x_planes[o, t])
+
+        load_x(0, 0)
+        cw_sb = sb("cw_sb", [P, PACK], F32)
+        nc.sync.dma_start(cw_sb[:], cw.rearrange("(p r) o -> p (r o)", r=PACK))
+        rw_sb = sb("rw_sb", [P, N], F32)
+        nc.sync.dma_start(rw_sb[:], rw)
+        load_x(0, 1)
+        wd_raw = sb("wd_raw", [P, PASSES, V], U32)
+        nc.sync.dma_start(wd_raw[:].bitcast(I32), wd_words.rearrange("o p n t -> p o (n t)").bitcast(I32))
+        for q in range(4):
+            nc.sync.dma_start(
+                wd_sc_raw[32 * q : 32 * q + 4 * PASSES, :].bitcast(I32),
+                wd_scales[:, 4 * q : 4 * q + 4, :].bitcast(I32),
+            )
+        load_x(0, 2)
+        load_x(0, 3)
+        for t in range(PACK):
+            load_x(1, t)
+        y_rows = y.rearrange("(p r) i -> p r i", r=PACK)
+        y_sb = [sb(f"y{h}", [P, PACK, H], F32) for h in range(HALVES)]
+        for h in range(HALVES):
+            nc.sync.dma_start(y_sb[h][:], y_rows[:, :, h * H : (h + 1) * H])
+        wv_sb = sb("wv_sb", [P, D], U32)
+        nc.sync.dma_start(wv_sb[:].bitcast(I32), wv_words[0].rearrange("p n t -> p (n t)").bitcast(I32))
+        for q in range(4):
+            nc.sync.dma_start(
+                wv_sc[32 * q : 32 * q + 4, :].bitcast(I32),
+                wv_scales[0, 4 * q : 4 * q + 4, :].bitcast(I32),
+            )
+
+        c_rows = sb("c_rows", [P, PACK, N], F32)
+        for r in range(PACK):
+            nc.scalar.activation(c_rows[:, r, :], rw_sb[:], COPY, scale=cw_sb[:, r : r + 1])
+        c_sb = [sb(f"c{h}", [P, H, PACK], F32) for h in range(HALVES)]
+        for h in range(HALVES):
+            nc.scalar.copy(
+                c_sb[h][:].rearrange("p (c i) r -> p c r i", i=4),
+                c_rows[:, :, h * H : (h + 1) * H].rearrange("p r (c i) -> p c r i", i=4),
+            )
+
+        xg0 = sb("xg0", [P, N, PACK], BF16)
+        wd_sb = sb("wd_sb", [P, PASSES, V], U32)
+        wd_sc = sb("wd_sc", [P, V], U8)
+        for t in range(PACK):
+            nc.vector.tensor_copy(xg0[:, :, t], x_sb[0][t][:].indirect(offsets[:]))
+            if t == 1:
+                nc.vector.tensor_copy(
+                    wd_sb[:].bitcast(I32).rearrange("p o (r s) -> p o s r", r=PACK),
+                    wd_raw[:].bitcast(I32).rearrange("p o (s r) -> p o s r", r=PACK),
+                )
+            if t == 2:
+                nc.vector.tensor_copy(
+                    wd_sc[:].rearrange("p (r s) -> p s r", r=PACK),
+                    wd_sc_raw[:].rearrange("p (s r) -> p s r", r=PACK),
+                )
+        xq0 = sb("xq0", [P, N], U32)
+        xs0 = sb("xs0", [P, N], U8)
+        nc.vector.quantize_mx(out=xq0[:].bitcast(E4M3X4), scales=xs0[:], in_=xg0[:].rearrange("p i t -> p (i t)"))
+
+        a_ps = [[psum.tile([P, H], F32, name=f"a{h}_{r}", tag=f"bank{PACK * h + r}") for r in range(PACK)] for h in range(HALVES)]
+
+        def score(o, h, r, codes, scales):
+            cols = slice(r * P, (r + 1) * P)
+            nc.tensor.matmul_mx(
+                out=a_ps[h][r][:],
+                lhsT=wd_sb[:, o, cols].bitcast(E4M3X4),
+                lhsT_scale=wd_sc[4 * o : P, cols],
+                rhs=codes.bitcast(E4M3X4),
+                rhs_scale=scales,
+                start=(o == 0),
+                stop=(o == PASSES - 1),
+            )
+
+        for h in range(HALVES):
+            for r in range(PACK):
+                score(0, h, r, xq0[:, h * H : (h + 1) * H], xs0[:, h * H : (h + 1) * H])
+
+        xg1 = [sb(f"xg1_{h}", [P, H, PACK], BF16) for h in range(HALVES)]
+        for t in range(PACK):
+            for h in range(HALVES):
+                nc.vector.tensor_copy(xg1[h][:, :, t], x_sb[1][t][:].indirect(offsets[:, h * H // 16 : (h + 1) * H // 16]))
+        for h in range(HALVES):
+            xq1 = sb(f"xq1_{h}", [P, H], U32)
+            xs1 = sb(f"xs1_{h}", [P, H], U8)
+            nc.vector.quantize_mx(out=xq1[:].bitcast(E4M3X4), scales=xs1[:], in_=xg1[h][:].rearrange("p i t -> p (i t)"))
+            for r in range(PACK):
+                score(1, h, r, xq1[:], xs1[:])
+
+        resid = [sb(f"resid{h}", [P, PACK, H], F32) for h in range(HALVES)]
+        for h in range(HALVES):
+            for r in range(PACK):
+                nc.vector.tensor_tensor(resid[h][:, r, :], a_ps[h][r][:], y_sb[h][:, r, :], ALU.subtract)
+        clipped = [sb(f"clipped{h}", [P, H, PACK], F32) for h in range(HALVES)]
+        for h in range(HALVES):
+            nc.vector.tensor_scalar(
+                clipped[h][:].rearrange("p (c i) r -> p c r i", i=4),
+                resid[h][:].rearrange("p r (c i) -> p c r i", i=4),
+                -1.0, 1.0, ALU.max, ALU.min,
+            )
+        g_sb = [sb(f"g{h}", [P, H * PACK], BF16) for h in range(HALVES)]
+        for h in range(HALVES):
+            nc.vector.tensor_tensor(
+                g_sb[h][:], clipped[h][:].rearrange("p i r -> p (i r)"), c_sb[h][:].rearrange("p i r -> p (i r)"), ALU.mult
+            )
+        gq = sb("gq", [P, N], U32)
+        gs = sb("gs", [P, N], U8)
+        for h in range(HALVES):
+            nc.vector.quantize_mx(out=gq[:, h * H : (h + 1) * H].bitcast(E5M2X4), scales=gs[:, h * H : (h + 1) * H], in_=g_sb[h][:])
+
+        for j in range(D_TILES):
+            cols = slice(j * P, (j + 1) * P)
+            dx_ps = psum.tile([P, N], F32, name=f"dx_ps{j}", tag=f"bank{j}")
+            nc.tensor.matmul_mx(
+                out=dx_ps[:],
+                lhsT=wv_sb[:, cols].bitcast(E4M3X4),
+                lhsT_scale=wv_sc[:, cols],
+                rhs=gq[:].bitcast(E5M2X4),
+                rhs_scale=gs[:],
+                start=True,
+                stop=True,
+            )
+            dx = sb(f"dx{j}", [P, N], F32)
+            nc.scalar.copy(dx[:], dx_ps[:])
+            window = windows[j % WINDOWS]
+            nc.vector.tensor_copy(window[:].indirect(offsets[:]), dx[:])
+            nc.sync.dma_start(out[cols, :], window[:])

@@ -1,6 +1,7 @@
 from contextlib import ExitStack
 
 import concourse.mybir as mybir
+from concourse.masks import make_identity
 
 N, T, D, V = 512, 2048, 1024, 512
 FLOPS = 2 * 2 * N * D * V
@@ -15,6 +16,7 @@ E4M3X4 = mybir.dt.float8_e4m3fn_x4
 E5M2X4 = mybir.dt.float8_e5m2_x4
 ALU = mybir.AluOpType
 COPY = mybir.ActivationFunctionType.Copy
+RELU = mybir.ActivationFunctionType.Relu
 
 P = 128
 PACK = 4
@@ -32,16 +34,21 @@ def tile_attend_gml_hub_kernel(tc, xT, wd_words, wd_scales, wv_words, wv_scales,
         keep = ctx.enter_context(tc.tile_pool(name="keep", bufs=1))
         psum = ctx.enter_context(tc.psum_pool(name="psum", bufs=1))
 
-        def sb(name, shape, dtype):
-            return keep.tile(shape, dtype, name=name, align_bytes=64)
+        def sb(name, shape, dtype, tag=None):
+            return keep.tile(shape, dtype, name=name, tag=tag or name, align_bytes=64)
 
         offsets = keep.tile([P, N // 16], U16, name="offsets")
-        nc.sync.dma_start(offsets[:], offs)
 
         wd_sc_raw = sb("wd_sc_raw", [P, V], U8)
         wv_sc = sb("wv_sc", [P, D], U8)
         nc.gpsimd.memset(wd_sc_raw[:].bitcast(I32), 0)
         nc.gpsimd.memset(wv_sc[:].bitcast(I32), 0)
+        gq = sb("gq", [P, H + N], U32)
+        gs = sb("gs", [P, H + N], U8)
+        nc.gpsimd.memset(gq[:, 0:H].bitcast(I32), 0)
+        nc.gpsimd.memset(gs[:, 0:H].bitcast(I32), 0)
+        ident = sb("ident", [P, P], F32)
+        make_identity(nc, ident[:])
         windows = [sb(f"window{w}", [P, T], F32) for w in range(WINDOWS)]
         for w in range(WINDOWS):
             nc.vector.memset(windows[w][:], 0.0)
@@ -53,10 +60,11 @@ def tile_attend_gml_hub_kernel(tc, xT, wd_words, wd_scales, wv_words, wv_scales,
             nc.sync.dma_start(x_sb[o][t][:], x_planes[o, t])
 
         load_x(0, 0)
+        nc.sync.dma_start(offsets[:], offs)
         cw_sb = sb("cw_sb", [P, PACK], F32)
         nc.sync.dma_start(cw_sb[:], cw.rearrange("(p r) o -> p (r o)", r=PACK))
-        rw_sb = sb("rw_sb", [P, N], F32)
-        nc.sync.dma_start(rw_sb[:], rw)
+        rw_col = sb("rw_col", [P, PACK], F32)
+        nc.sync.dma_start(rw_col[:], rw[0:1, :].rearrange("o (p j) -> p (o j)", j=PACK))
         load_x(0, 1)
         wd_raw = sb("wd_raw", [P, PASSES, V], U32)
         nc.sync.dma_start(wd_raw[:].bitcast(I32), wd_words.rearrange("o p n t -> p o (n t)").bitcast(I32))
@@ -81,9 +89,17 @@ def tile_attend_gml_hub_kernel(tc, xT, wd_words, wd_scales, wv_words, wv_scales,
                 wv_scales[0, 4 * q : 4 * q + 4, :].bitcast(I32),
             )
 
+        rw_ps = psum.tile([P, PACK, P], F32, name="rw_ps", tag="bank0")
+        for j in range(PACK):
+            nc.tensor.transpose(rw_ps[:, j, :], rw_col[:, j : j + 1].to_broadcast([P, P]), ident[:])
         c_rows = sb("c_rows", [P, PACK, N], F32)
         for r in range(PACK):
-            nc.scalar.activation(c_rows[:, r, :], rw_sb[:], COPY, scale=cw_sb[:, r : r + 1])
+            nc.scalar.activation(
+                c_rows[:, r, :].rearrange("p (s j) -> p s j", j=PACK),
+                rw_ps[:].rearrange("p j s -> p s j"),
+                COPY,
+                scale=cw_sb[:, r : r + 1],
+            )
         c_sb = [sb(f"c{h}", [P, H, PACK], F32) for h in range(HALVES)]
         for h in range(HALVES):
             nc.scalar.copy(
@@ -91,11 +107,12 @@ def tile_attend_gml_hub_kernel(tc, xT, wd_words, wd_scales, wv_words, wv_scales,
                 c_rows[:, :, h * H : (h + 1) * H].rearrange("p r (c i) -> p c r i", i=4),
             )
 
+        xf0 = sb("xf0", [P, PACK, N], F32)
         xg0 = sb("xg0", [P, N, PACK], BF16)
         wd_sb = sb("wd_sb", [P, PASSES, V], U32)
         wd_sc = sb("wd_sc", [P, V], U8)
         for t in range(PACK):
-            nc.vector.tensor_copy(xg0[:, :, t], x_sb[0][t][:].indirect(offsets[:]))
+            nc.vector.tensor_copy(xf0[:, t, :], x_sb[0][t][:].indirect(offsets[:]))
             if t == 1:
                 nc.vector.tensor_copy(
                     wd_sb[:].bitcast(I32).rearrange("p o (r s) -> p o s r", r=PACK),
@@ -106,6 +123,10 @@ def tile_attend_gml_hub_kernel(tc, xT, wd_words, wd_scales, wv_words, wv_scales,
                     wd_sc[:].rearrange("p (r s) -> p s r", r=PACK),
                     wd_sc_raw[:].rearrange("p (s r) -> p s r", r=PACK),
                 )
+        nc.scalar.copy(
+            xg0[:].rearrange("p (c i) t -> p c t i", i=4),
+            xf0[:].rearrange("p t (c i) -> p c t i", i=4),
+        )
         xq0 = sb("xq0", [P, N], U32)
         xs0 = sb("xs0", [P, N], U8)
         nc.vector.quantize_mx(out=xq0[:].bitcast(E4M3X4), scales=xs0[:], in_=xg0[:].rearrange("p i t -> p (i t)"))
@@ -129,7 +150,15 @@ def tile_attend_gml_hub_kernel(tc, xT, wd_words, wd_scales, wv_words, wv_scales,
                 score(0, h, r, xq0[:, h * H : (h + 1) * H], xs0[:, h * H : (h + 1) * H])
 
         xg1 = [sb(f"xg1_{h}", [P, H, PACK], BF16) for h in range(HALVES)]
-        for t in range(PACK):
+        xf1 = sb("xf1", [P, 2, N], F32)
+        for t in range(2):
+            nc.vector.tensor_copy(xf1[:, t, :], x_sb[1][t][:].indirect(offsets[:]))
+        for h in range(HALVES):
+            nc.scalar.copy(
+                xg1[h][:, :, 0:2].rearrange("p (c i) t -> p c t i", i=4),
+                xf1[:, :, h * H : (h + 1) * H].rearrange("p t (c i) -> p c t i", i=4),
+            )
+        for t in range(2, PACK):
             for h in range(HALVES):
                 nc.vector.tensor_copy(xg1[h][:, :, t], x_sb[1][t][:].indirect(offsets[:, h * H // 16 : (h + 1) * H // 16]))
         for h in range(HALVES):
@@ -143,37 +172,59 @@ def tile_attend_gml_hub_kernel(tc, xT, wd_words, wd_scales, wv_words, wv_scales,
         for h in range(HALVES):
             for r in range(PACK):
                 nc.vector.tensor_tensor(resid[h][:, r, :], a_ps[h][r][:], y_sb[h][:, r, :], ALU.subtract)
-        clipped = [sb(f"clipped{h}", [P, H, PACK], F32) for h in range(HALVES)]
-        for h in range(HALVES):
-            nc.vector.tensor_scalar(
-                clipped[h][:].rearrange("p (c i) r -> p c r i", i=4),
-                resid[h][:].rearrange("p r (c i) -> p c r i", i=4),
-                -1.0, 1.0, ALU.max, ALU.min,
-            )
         g_sb = [sb(f"g{h}", [P, H * PACK], BF16) for h in range(HALVES)]
-        for h in range(HALVES):
-            nc.vector.tensor_tensor(
-                g_sb[h][:], clipped[h][:].rearrange("p i r -> p (i r)"), c_sb[h][:].rearrange("p i r -> p (i r)"), ALU.mult
-            )
-        gq = sb("gq", [P, N], U32)
-        gs = sb("gs", [P, N], U8)
-        for h in range(HALVES):
-            nc.vector.quantize_mx(out=gq[:, h * H : (h + 1) * H].bitcast(E5M2X4), scales=gs[:, h * H : (h + 1) * H], in_=g_sb[h][:])
 
-        for j in range(D_TILES):
+        def quantize_g(h):
+            cols = slice((h + 1) * H, (h + 2) * H)
+            nc.vector.quantize_mx(out=gq[:, cols].bitcast(E5M2X4), scales=gs[:, cols], in_=g_sb[h][:])
+
+        clipped = sb("clipped", [P, H, PACK], F32)
+        nc.vector.tensor_scalar(
+            clipped[:].rearrange("p (c i) r -> p c r i", i=4),
+            resid[0][:].rearrange("p r (c i) -> p c r i", i=4),
+            -1.0, 1.0, ALU.max, ALU.min,
+        )
+        below = sb("below", [P, PACK, H], F32)
+        for r in range(PACK):
+            nc.scalar.activation(below[:, r, :], resid[1][:, r, :], RELU, bias=1.0, scale=-1.0)
+        shifted = sb("shifted", [P, H, PACK], F32)
+        nc.scalar.activation(
+            shifted[:].rearrange("p (c i) r -> p c r i", i=4),
+            below[:].rearrange("p r (c i) -> p c r i", i=4),
+            RELU, bias=2.0, scale=-1.0,
+        )
+        nc.vector.tensor_tensor(
+            g_sb[0][:], clipped[:].rearrange("p i r -> p (i r)"), c_sb[0][:].rearrange("p i r -> p (i r)"), ALU.mult
+        )
+        quantize_g(0)
+        nc.vector.scalar_tensor_tensor(
+            g_sb[1][:], shifted[:].rearrange("p i r -> p (i r)"), -1.0, c_sb[1][:].rearrange("p i r -> p (i r)"), ALU.add, ALU.mult
+        )
+        quantize_g(1)
+
+        def back(j, first, bank):
             cols = slice(j * P, (j + 1) * P)
-            dx_ps = psum.tile([P, N], F32, name=f"dx_ps{j}", tag=f"bank{j}")
+            dx_ps = psum.tile([P, N], F32, name=f"dx_ps{j}_{first}", tag=f"bank{bank}")
             nc.tensor.matmul_mx(
                 out=dx_ps[:],
                 lhsT=wv_sb[:, cols].bitcast(E4M3X4),
                 lhsT_scale=wv_sc[:, cols],
-                rhs=gq[:].bitcast(E5M2X4),
-                rhs_scale=gs[:],
+                rhs=gq[:, first : first + N].bitcast(E5M2X4),
+                rhs_scale=gs[:, first : first + N],
                 start=True,
                 stop=True,
             )
-            dx = sb(f"dx{j}", [P, N], F32)
-            nc.scalar.copy(dx[:], dx_ps[:])
-            window = windows[j % WINDOWS]
-            nc.vector.tensor_copy(window[:].indirect(offsets[:]), dx[:])
-            nc.sync.dma_start(out[cols, :], window[:])
+            return dx_ps
+
+        def place(j, name, src, lo, hi, tag=None):
+            dx = sb(name, [P, hi - lo], F32, tag)
+            nc.scalar.copy(dx[:], src)
+            nc.vector.tensor_copy(windows[j % WINDOWS][:].indirect(offsets[:, lo // 16 : hi // 16]), dx[:])
+
+        early = back(0, 0, 0)
+        place(0, "dx_early", early[:, H:N], 0, H, tag="shifted")
+        for j in range(D_TILES):
+            dx_ps = back(j, H, (j + 1) % D_TILES)
+            lo = H if j == 0 else 0
+            place(j, f"dx{j}", dx_ps[:, lo:N], lo, N)
+            nc.sync.dma_start(out[j * P : (j + 1) * P, :], windows[j % WINDOWS][:])

@@ -172,35 +172,44 @@ def tile_attend_gml_hub_kernel(tc, xT, wd_words, wd_scales, wv_words, wv_scales,
         for h in range(HALVES):
             for r in range(PACK):
                 nc.vector.tensor_tensor(resid[h][:, r, :], a_ps[h][r][:], y_sb[h][:, r, :], ALU.subtract)
-        g_sb = [sb(f"g{h}", [P, H * PACK], BF16) for h in range(HALVES)]
+        quarters = HALVES * 2
+        Q = N // quarters
+        g_sb = [sb(f"g{u}", [P, Q * PACK], BF16) for u in range(quarters)]
 
-        def quantize_g(h):
-            cols = slice((h + 1) * H, (h + 2) * H)
-            nc.vector.quantize_mx(out=gq[:, cols].bitcast(E5M2X4), scales=gs[:, cols], in_=g_sb[h][:])
+        def quantize_g(u):
+            cols = slice(H + u * Q, H + (u + 1) * Q)
+            nc.vector.quantize_mx(out=gq[:, cols].bitcast(E5M2X4), scales=gs[:, cols], in_=g_sb[u][:])
 
-        clipped = sb("clipped", [P, H, PACK], F32)
-        nc.vector.tensor_scalar(
-            clipped[:].rearrange("p (c i) r -> p c r i", i=4),
-            resid[0][:].rearrange("p r (c i) -> p c r i", i=4),
-            -1.0, 1.0, ALU.max, ALU.min,
-        )
+        def c_of(u):
+            return c_sb[u // 2][:, (u % 2) * Q : (u % 2 + 1) * Q, :].rearrange("p i r -> p (i r)")
+
+        clipped = [sb(f"clipped{u}", [P, Q, PACK], F32) for u in range(2)]
+        for u in range(2):
+            nc.vector.tensor_scalar(
+                clipped[u][:].rearrange("p (c i) r -> p c r i", i=4),
+                resid[0][:, :, u * Q : (u + 1) * Q].rearrange("p r (c i) -> p c r i", i=4),
+                -1.0, 1.0, ALU.max, ALU.min,
+            )
         below = sb("below", [P, PACK, H], F32)
         for r in range(PACK):
             nc.scalar.activation(below[:, r, :], resid[1][:, r, :], RELU, bias=1.0, scale=-1.0)
-        shifted = sb("shifted", [P, H, PACK], F32)
-        nc.scalar.activation(
-            shifted[:].rearrange("p (c i) r -> p c r i", i=4),
-            below[:].rearrange("p r (c i) -> p c r i", i=4),
-            RELU, bias=2.0, scale=-1.0,
-        )
-        nc.vector.tensor_tensor(
-            g_sb[0][:], clipped[:].rearrange("p i r -> p (i r)"), c_sb[0][:].rearrange("p i r -> p (i r)"), ALU.mult
-        )
-        quantize_g(0)
-        nc.vector.scalar_tensor_tensor(
-            g_sb[1][:], shifted[:].rearrange("p i r -> p (i r)"), -1.0, c_sb[1][:].rearrange("p i r -> p (i r)"), ALU.add, ALU.mult
-        )
-        quantize_g(1)
+        shifted = [sb(f"shifted{u}", [P, Q, PACK], F32) for u in range(2)]
+        for u in range(2):
+            nc.scalar.activation(
+                shifted[u][:].rearrange("p (c i) r -> p c r i", i=4),
+                below[:, :, u * Q : (u + 1) * Q].rearrange("p r (c i) -> p c r i", i=4),
+                RELU, bias=2.0, scale=-1.0,
+            )
+        for u in range(2):
+            nc.vector.tensor_tensor(g_sb[u][:], clipped[u][:].rearrange("p i r -> p (i r)"), c_of(u), ALU.mult)
+        for u in range(2):
+            quantize_g(u)
+        for u in range(2):
+            nc.vector.scalar_tensor_tensor(
+                g_sb[2 + u][:], shifted[u][:].rearrange("p i r -> p (i r)"), -1.0, c_of(2 + u), ALU.add, ALU.mult
+            )
+        for u in range(2):
+            quantize_g(2 + u)
 
         def back(j, first, bank):
             cols = slice(j * P, (j + 1) * P)
@@ -222,7 +231,7 @@ def tile_attend_gml_hub_kernel(tc, xT, wd_words, wd_scales, wv_words, wv_scales,
             nc.vector.tensor_copy(windows[j % WINDOWS][:].indirect(offsets[:, lo // 16 : hi // 16]), dx[:])
 
         early = back(0, 0, 0)
-        place(0, "dx_early", early[:, H:N], 0, H, tag="shifted")
+        place(0, "dx_early", early[:, H:N], 0, H, tag="shifted1")
         for j in range(D_TILES):
             dx_ps = back(j, H, (j + 1) % D_TILES)
             lo = H if j == 0 else 0

@@ -53,19 +53,22 @@ def tile_attend_gml_hub_kernel(tc, xT, wd_words, wd_scales, wv_words, wv_scales,
         for w in range(WINDOWS):
             nc.vector.memset(windows[w][:], 0.0)
 
-        x_planes = xT.rearrange("(o p t) n -> o t p n", o=PASSES, t=PACK)
-        x_sb = [[sb(f"x{o}_{t}", [P, T], F32) for t in range(PACK)] for o in range(PASSES)]
+        x_planes = xT.rearrange("(o p t) n -> o p t n", o=PASSES, t=PACK)
+        x_sb = {}
 
-        def load_x(o, t):
-            nc.sync.dma_start(x_sb[o][t][:], x_planes[o, t])
+        def load_x(o, t, count):
+            tile = sb(f"x{o}_{t}", [P, count, T], F32)
+            nc.sync.dma_start(tile[:], x_planes[o, :, t : t + count, :])
+            for e in range(count):
+                x_sb[o, t + e] = tile[:, e, :]
 
-        load_x(0, 0)
+        load_x(0, 0, 2)
         nc.sync.dma_start(offsets[:], offs)
         cw_sb = sb("cw_sb", [P, PACK], F32)
         nc.sync.dma_start(cw_sb[:], cw.rearrange("(p r) o -> p (r o)", r=PACK))
         rw_col = sb("rw_col", [P, PACK], F32)
         nc.sync.dma_start(rw_col[:], rw[0:1, :].rearrange("o (p j) -> p (o j)", j=PACK))
-        load_x(0, 1)
+        load_x(0, 2, 2)
         wd_raw = sb("wd_raw", [P, PASSES, V], U32)
         nc.sync.dma_start(wd_raw[:].bitcast(I32), wd_words.rearrange("o p n t -> p o (n t)").bitcast(I32))
         for q in range(4):
@@ -73,10 +76,9 @@ def tile_attend_gml_hub_kernel(tc, xT, wd_words, wd_scales, wv_words, wv_scales,
                 wd_sc_raw[32 * q : 32 * q + 4 * PASSES, :].bitcast(I32),
                 wd_scales[:, 4 * q : 4 * q + 4, :].bitcast(I32),
             )
-        load_x(0, 2)
-        load_x(0, 3)
-        for t in range(PACK):
-            load_x(1, t)
+        load_x(1, 0, 2)
+        load_x(1, 2, 1)
+        load_x(1, 3, 1)
         y_rows = y.rearrange("(p r) i -> p r i", r=PACK)
         y_sb = [sb(f"y{h}", [P, PACK, H], F32) for h in range(HALVES)]
         for h in range(HALVES):
@@ -112,7 +114,7 @@ def tile_attend_gml_hub_kernel(tc, xT, wd_words, wd_scales, wv_words, wv_scales,
         wd_sb = sb("wd_sb", [P, PASSES, V], U32)
         wd_sc = sb("wd_sc", [P, V], U8)
         for t in range(PACK):
-            nc.vector.tensor_copy(xf0[:, t, :], x_sb[0][t][:].indirect(offsets[:]))
+            nc.vector.tensor_copy(xf0[:, t, :], x_sb[0, t].indirect(offsets[:]))
             if t == 1:
                 nc.vector.tensor_copy(
                     wd_sb[:].bitcast(I32).rearrange("p o (r s) -> p o s r", r=PACK),
@@ -152,7 +154,7 @@ def tile_attend_gml_hub_kernel(tc, xT, wd_words, wd_scales, wv_words, wv_scales,
         xg1 = [sb(f"xg1_{h}", [P, H, PACK], BF16) for h in range(HALVES)]
         xf1 = sb("xf1", [P, 2, N], F32)
         for t in range(2):
-            nc.vector.tensor_copy(xf1[:, t, :], x_sb[1][t][:].indirect(offsets[:]))
+            nc.vector.tensor_copy(xf1[:, t, :], x_sb[1, t].indirect(offsets[:]))
         for h in range(HALVES):
             nc.scalar.copy(
                 xg1[h][:, :, 0:2].rearrange("p (c i) t -> p c t i", i=4),
@@ -160,7 +162,7 @@ def tile_attend_gml_hub_kernel(tc, xT, wd_words, wd_scales, wv_words, wv_scales,
             )
         for t in range(2, PACK):
             for h in range(HALVES):
-                nc.vector.tensor_copy(xg1[h][:, :, t], x_sb[1][t][:].indirect(offsets[:, h * H // 16 : (h + 1) * H // 16]))
+                nc.vector.tensor_copy(xg1[h][:, :, t], x_sb[1, t].indirect(offsets[:, h * H // 16 : (h + 1) * H // 16]))
         for h in range(HALVES):
             xq1 = sb(f"xq1_{h}", [P, H], U32)
             xs1 = sb(f"xs1_{h}", [P, H], U8)

@@ -16,7 +16,6 @@ E4M3X4 = mybir.dt.float8_e4m3fn_x4
 E5M2X4 = mybir.dt.float8_e5m2_x4
 ALU = mybir.AluOpType
 COPY = mybir.ActivationFunctionType.Copy
-RELU = mybir.ActivationFunctionType.Relu
 
 P = 128
 PACK = 4
@@ -24,8 +23,9 @@ K_PASS = P * PACK
 PASSES = D // K_PASS
 HALVES = 2
 H = N // HALVES
+Q = H // 2
 D_TILES = D // P
-WINDOWS = 3
+EARLY = 4
 
 
 def tile_attend_gml_hub_kernel(tc, xT, wd_words, wd_scales, wv_words, wv_scales, y, cw, rw, offs, out):
@@ -39,6 +39,9 @@ def tile_attend_gml_hub_kernel(tc, xT, wd_words, wd_scales, wv_words, wv_scales,
 
         offsets = keep.tile([P, N // 16], U16, name="offsets")
 
+        def listed(lo, hi):
+            return offsets[:, lo // 16 : hi // 16]
+
         wd_sc_raw = sb("wd_sc_raw", [P, V], U8)
         wv_sc = sb("wv_sc", [P, D], U8)
         nc.gpsimd.memset(wd_sc_raw[:].bitcast(I32), 0)
@@ -49,9 +52,10 @@ def tile_attend_gml_hub_kernel(tc, xT, wd_words, wd_scales, wv_words, wv_scales,
         nc.gpsimd.memset(gs[:, 0:H].bitcast(I32), 0)
         ident = sb("ident", [P, P], F32)
         make_identity(nc, ident[:])
-        windows = [sb(f"window{w}", [P, T], F32) for w in range(WINDOWS)]
-        for w in range(WINDOWS):
+        windows = [sb(f"window{w}", [P, T], F32) for w in range(EARLY)]
+        for w in range(EARLY - 1):
             nc.vector.memset(windows[w][:], 0.0)
+        nc.gpsimd.memset(windows[EARLY - 1][:], 0.0)
 
         x_planes = xT.rearrange("(o p t) n -> o p t n", o=PASSES, t=PACK)
         x_sb = {}
@@ -62,6 +66,11 @@ def tile_attend_gml_hub_kernel(tc, xT, wd_words, wd_scales, wv_words, wv_scales,
             for e in range(count):
                 x_sb[o, t + e] = tile[:, e, :]
 
+        wd_raw = [sb(f"wd_raw{o}", [P, V], U32) for o in range(PASSES)]
+
+        def load_wd(o):
+            nc.sync.dma_start(wd_raw[o][:].bitcast(I32), wd_words[o].rearrange("p n t -> p (n t)").bitcast(I32))
+
         load_x(0, 0, 2)
         nc.sync.dma_start(offsets[:], offs)
         cw_sb = sb("cw_sb", [P, PACK], F32)
@@ -69,8 +78,7 @@ def tile_attend_gml_hub_kernel(tc, xT, wd_words, wd_scales, wv_words, wv_scales,
         rw_col = sb("rw_col", [P, PACK], F32)
         nc.sync.dma_start(rw_col[:], rw[0:1, :].rearrange("o (p j) -> p (o j)", j=PACK))
         load_x(0, 2, 2)
-        wd_raw = sb("wd_raw", [P, PASSES, V], U32)
-        nc.sync.dma_start(wd_raw[:].bitcast(I32), wd_words.rearrange("o p n t -> p o (n t)").bitcast(I32))
+        load_wd(0)
         for q in range(4):
             nc.sync.dma_start(
                 wd_sc_raw[32 * q : 32 * q + 4 * PASSES, :].bitcast(I32),
@@ -79,6 +87,7 @@ def tile_attend_gml_hub_kernel(tc, xT, wd_words, wd_scales, wv_words, wv_scales,
         load_x(1, 0, 2)
         load_x(1, 2, 1)
         load_x(1, 3, 1)
+        load_wd(1)
         y_rows = y.rearrange("(p r) i -> p r i", r=PACK)
         y_sb = [sb(f"y{h}", [P, PACK, H], F32) for h in range(HALVES)]
         for h in range(HALVES):
@@ -109,22 +118,24 @@ def tile_attend_gml_hub_kernel(tc, xT, wd_words, wd_scales, wv_words, wv_scales,
                 c_rows[:, :, h * H : (h + 1) * H].rearrange("p r (c i) -> p c r i", i=4),
             )
 
+        wd_sb = [sb(f"wd_sb{o}", [P, V], U32) for o in range(PASSES)]
+        wd_sc = sb("wd_sc", [P, V], U8)
+
+        def deal_wd(o):
+            nc.vector.tensor_copy(
+                wd_sb[o][:].bitcast(I32).rearrange("p (r s) -> p s r", r=PACK),
+                wd_raw[o][:].bitcast(I32).rearrange("p (s r) -> p s r", r=PACK),
+            )
+
         xf0 = sb("xf0", [P, PACK, N], F32)
         xg0 = sb("xg0", [P, N, PACK], BF16)
-        wd_sb = sb("wd_sb", [P, PASSES, V], U32)
-        wd_sc = sb("wd_sc", [P, V], U8)
         for t in range(PACK):
             nc.vector.tensor_copy(xf0[:, t, :], x_sb[0, t].indirect(offsets[:]))
-            if t == 1:
-                nc.vector.tensor_copy(
-                    wd_sb[:].bitcast(I32).rearrange("p o (r s) -> p o s r", r=PACK),
-                    wd_raw[:].bitcast(I32).rearrange("p o (s r) -> p o s r", r=PACK),
-                )
-            if t == 2:
-                nc.vector.tensor_copy(
-                    wd_sc[:].rearrange("p (r s) -> p s r", r=PACK),
-                    wd_sc_raw[:].rearrange("p (s r) -> p s r", r=PACK),
-                )
+        deal_wd(0)
+        nc.vector.tensor_copy(
+            wd_sc[:].rearrange("p (r s) -> p s r", r=PACK),
+            wd_sc_raw[:].rearrange("p (s r) -> p s r", r=PACK),
+        )
         nc.scalar.copy(
             xg0[:].rearrange("p (c i) t -> p c t i", i=4),
             xf0[:].rearrange("p t (c i) -> p c t i", i=4),
@@ -135,21 +146,21 @@ def tile_attend_gml_hub_kernel(tc, xT, wd_words, wd_scales, wv_words, wv_scales,
 
         a_ps = [[psum.tile([P, H], F32, name=f"a{h}_{r}", tag=f"bank{PACK * h + r}") for r in range(PACK)] for h in range(HALVES)]
 
-        def score(o, h, r, codes, scales):
-            cols = slice(r * P, (r + 1) * P)
-            nc.tensor.matmul_mx(
-                out=a_ps[h][r][:],
-                lhsT=wd_sb[:, o, cols].bitcast(E4M3X4),
-                lhsT_scale=wd_sc[4 * o : P, cols],
-                rhs=codes.bitcast(E4M3X4),
-                rhs_scale=scales,
-                start=(o == 0),
-                stop=(o == PASSES - 1),
-            )
+        def score(o, h, codes, scales):
+            for r in range(PACK):
+                cols = slice(r * P, (r + 1) * P)
+                nc.tensor.matmul_mx(
+                    out=a_ps[h][r][:],
+                    lhsT=wd_sb[o][:, cols].bitcast(E4M3X4),
+                    lhsT_scale=wd_sc[4 * o : P, cols],
+                    rhs=codes.bitcast(E4M3X4),
+                    rhs_scale=scales,
+                    start=(o == 0),
+                    stop=(o == PASSES - 1),
+                )
 
         for h in range(HALVES):
-            for r in range(PACK):
-                score(0, h, r, xq0[:, h * H : (h + 1) * H], xs0[:, h * H : (h + 1) * H])
+            score(0, h, xq0[:, h * H : (h + 1) * H], xs0[:, h * H : (h + 1) * H])
 
         xg1 = [sb(f"xg1_{h}", [P, H, PACK], BF16) for h in range(HALVES)]
         xf1 = sb("xf1", [P, 2, N], F32)
@@ -160,58 +171,68 @@ def tile_attend_gml_hub_kernel(tc, xT, wd_words, wd_scales, wv_words, wv_scales,
                 xg1[h][:, :, 0:2].rearrange("p (c i) t -> p c t i", i=4),
                 xf1[:, :, h * H : (h + 1) * H].rearrange("p t (c i) -> p c t i", i=4),
             )
-        for t in range(2, PACK):
-            for h in range(HALVES):
-                nc.vector.tensor_copy(xg1[h][:, :, t], x_sb[1, t].indirect(offsets[:, h * H // 16 : (h + 1) * H // 16]))
-        for h in range(HALVES):
+
+        def gather_late(t, tag=None):
+            late = sb(f"late{t}", [P, H], F32, tag)
+            nc.vector.tensor_copy(late[:], x_sb[1, t].indirect(listed(H, N)))
+            nc.scalar.copy(xg1[1][:, :, t], late[:])
+
+        def quantize_x1(h):
             xq1 = sb(f"xq1_{h}", [P, H], U32)
             xs1 = sb(f"xs1_{h}", [P, H], U8)
             nc.vector.quantize_mx(out=xq1[:].bitcast(E4M3X4), scales=xs1[:], in_=xg1[h][:].rearrange("p i t -> p (i t)"))
-            for r in range(PACK):
-                score(1, h, r, xq1[:], xs1[:])
+            score(1, h, xq1[:], xs1[:])
+
+        nc.vector.tensor_copy(xg1[0][:, :, 2], x_sb[1, 2].indirect(listed(0, H)))
+        gather_late(2)
+        nc.vector.tensor_copy(xg1[0][:, :, 3], x_sb[1, 3].indirect(listed(0, H)))
+        deal_wd(1)
+        quantize_x1(0)
+        gather_late(3, tag="wd_raw1")
 
         resid = [sb(f"resid{h}", [P, PACK, H], F32) for h in range(HALVES)]
-        for h in range(HALVES):
+
+        def residual(h):
             for r in range(PACK):
                 nc.vector.tensor_tensor(resid[h][:, r, :], a_ps[h][r][:], y_sb[h][:, r, :], ALU.subtract)
-        quarters = HALVES * 2
-        Q = N // quarters
-        g_sb = [sb(f"g{u}", [P, Q * PACK], BF16) for u in range(quarters)]
 
-        def quantize_g(u):
-            cols = slice(H + u * Q, H + (u + 1) * Q)
-            nc.vector.quantize_mx(out=gq[:, cols].bitcast(E5M2X4), scales=gs[:, cols], in_=g_sb[u][:])
-
-        def c_of(u):
-            return c_sb[u // 2][:, (u % 2) * Q : (u % 2 + 1) * Q, :].rearrange("p i r -> p (i r)")
-
-        clipped = [sb(f"clipped{u}", [P, Q, PACK], F32) for u in range(2)]
-        for u in range(2):
+        def clip(dst, src):
             nc.vector.tensor_scalar(
-                clipped[u][:].rearrange("p (c i) r -> p c r i", i=4),
-                resid[0][:, :, u * Q : (u + 1) * Q].rearrange("p r (c i) -> p c r i", i=4),
+                dst.rearrange("p (c i) r -> p c r i", i=4),
+                src.rearrange("p r (c i) -> p c r i", i=4),
                 -1.0, 1.0, ALU.max, ALU.min,
             )
-        below = sb("below", [P, PACK, H], F32)
-        for r in range(PACK):
-            nc.scalar.activation(below[:, r, :], resid[1][:, r, :], RELU, bias=1.0, scale=-1.0)
-        shifted = [sb(f"shifted{u}", [P, Q, PACK], F32) for u in range(2)]
+
+        def quantize_g(lo, hi, g):
+            cols = slice(H + lo, H + hi)
+            nc.vector.quantize_mx(out=gq[:, cols].bitcast(E5M2X4), scales=gs[:, cols], in_=g)
+
+        residual(0)
+        quantize_x1(1)
+        clipped = [sb(f"clipped{u}", [P, Q, PACK], F32) for u in range(2)]
+        g_first = [sb(f"g{u}", [P, Q * PACK], BF16) for u in range(2)]
         for u in range(2):
-            nc.scalar.activation(
-                shifted[u][:].rearrange("p (c i) r -> p c r i", i=4),
-                below[:, :, u * Q : (u + 1) * Q].rearrange("p r (c i) -> p c r i", i=4),
-                RELU, bias=2.0, scale=-1.0,
+            clip(clipped[u][:], resid[0][:, :, u * Q : (u + 1) * Q])
+        for u in range(2):
+            nc.vector.tensor_tensor(
+                g_first[u][:],
+                clipped[u][:].rearrange("p i r -> p (i r)"),
+                c_sb[0][:, u * Q : (u + 1) * Q, :].rearrange("p i r -> p (i r)"),
+                ALU.mult,
             )
         for u in range(2):
-            nc.vector.tensor_tensor(g_sb[u][:], clipped[u][:].rearrange("p i r -> p (i r)"), c_of(u), ALU.mult)
-        for u in range(2):
-            quantize_g(u)
-        for u in range(2):
-            nc.vector.scalar_tensor_tensor(
-                g_sb[2 + u][:], shifted[u][:].rearrange("p i r -> p (i r)"), -1.0, c_of(2 + u), ALU.add, ALU.mult
-            )
-        for u in range(2):
-            quantize_g(2 + u)
+            quantize_g(u * Q, (u + 1) * Q, g_first[u][:])
+
+        residual(1)
+        clipped_second = sb("clipped_second", [P, H, PACK], F32)
+        clip(clipped_second[:], resid[1][:])
+        g_second = sb("g_second", [P, H * PACK], BF16)
+        nc.gpsimd.tensor_tensor(
+            g_second[:],
+            clipped_second[:].rearrange("p i r -> p (i r)"),
+            c_sb[1][:].rearrange("p i r -> p (i r)"),
+            ALU.mult,
+        )
 
         def back(j, first, bank):
             cols = slice(j * P, (j + 1) * P)
@@ -230,12 +251,15 @@ def tile_attend_gml_hub_kernel(tc, xT, wd_words, wd_scales, wv_words, wv_scales,
         def place(j, name, src, lo, hi, tag=None):
             dx = sb(name, [P, hi - lo], F32, tag)
             nc.scalar.copy(dx[:], src)
-            nc.vector.tensor_copy(windows[j % WINDOWS][:].indirect(offsets[:, lo // 16 : hi // 16]), dx[:])
+            nc.vector.tensor_copy(windows[j % EARLY][:].indirect(listed(lo, hi)), dx[:])
 
-        early = back(0, 0, 0)
-        place(0, "dx_early", early[:, H:N], 0, H, tag="shifted1")
+        early = [back(j, 0, j) for j in range(EARLY)]
+        for j in range(EARLY - 1):
+            place(j, f"dx_early{j}", early[j][:, H:N], 0, H)
+        quantize_g(H, N, g_second[:])
+        place(EARLY - 1, "dx_early_last", early[EARLY - 1][:, H:N], 0, H, tag="clipped_second")
         for j in range(D_TILES):
-            dx_ps = back(j, H, (j + 1) % D_TILES)
-            lo = H if j == 0 else 0
+            dx_ps = back(j, H, (j + EARLY) % D_TILES)
+            lo = H if j < EARLY else 0
             place(j, f"dx{j}", dx_ps[:, lo:N], lo, N)
-            nc.sync.dma_start(out[j * P : (j + 1) * P, :], windows[j % WINDOWS][:])
+            nc.sync.dma_start(out[j * P : (j + 1) * P, :], windows[j % EARLY][:])

@@ -32,6 +32,7 @@ def tile_attend_gml_hub_kernel(tc, xT, wd_words, wd_scales, wv_words, wv_scales,
     nc = tc.nc
     with ExitStack() as ctx:
         keep = ctx.enter_context(tc.tile_pool(name="keep", bufs=1))
+        shared = ctx.enter_context(tc.tile_pool(name="shared", bufs=1))
         psum = ctx.enter_context(tc.psum_pool(name="psum", bufs=1))
 
         def sb(name, shape, dtype, tag=None):
@@ -66,7 +67,10 @@ def tile_attend_gml_hub_kernel(tc, xT, wd_words, wd_scales, wv_words, wv_scales,
             for e in range(count):
                 x_sb[o, t + e] = tile[:, e, :]
 
-        wd_raw = [sb(f"wd_raw{o}", [P, V], U32) for o in range(PASSES)]
+        wd_raw = [
+            sb("wd_raw0", [P, V], U32),
+            shared.tile([P, V], U32, name="wd_raw1", align_bytes=64, offset=0),
+        ]
 
         def load_wd(o):
             nc.sync.dma_start(wd_raw[o][:].bitcast(I32), wd_words[o].rearrange("p n t -> p (n t)").bitcast(I32))
@@ -84,7 +88,8 @@ def tile_attend_gml_hub_kernel(tc, xT, wd_words, wd_scales, wv_words, wv_scales,
                 wd_sc_raw[32 * q : 32 * q + 4 * PASSES, :].bitcast(I32),
                 wd_scales[:, 4 * q : 4 * q + 4, :].bitcast(I32),
             )
-        load_x(1, 0, 2)
+        load_x(1, 0, 1)
+        load_x(1, 1, 1)
         load_x(1, 2, 1)
         load_x(1, 3, 1)
         load_wd(1)
@@ -140,7 +145,7 @@ def tile_attend_gml_hub_kernel(tc, xT, wd_words, wd_scales, wv_words, wv_scales,
             xg0[:].rearrange("p (c i) t -> p c t i", i=4),
             xf0[:].rearrange("p t (c i) -> p c t i", i=4),
         )
-        xq0 = sb("xq0", [P, N], U32)
+        xq0 = sb("xq0", [P, N], U32, tag="x1_1")
         xs0 = sb("xs0", [P, N], U8)
         nc.vector.quantize_mx(out=xq0[:].bitcast(E4M3X4), scales=xs0[:], in_=xg0[:].rearrange("p i t -> p (i t)"))
 
@@ -172,23 +177,24 @@ def tile_attend_gml_hub_kernel(tc, xT, wd_words, wd_scales, wv_words, wv_scales,
                 xf1[:, :, h * H : (h + 1) * H].rearrange("p t (c i) -> p c t i", i=4),
             )
 
-        def gather_late(t, tag=None):
-            late = sb(f"late{t}", [P, H], F32, tag)
-            nc.vector.tensor_copy(late[:], x_sb[1, t].indirect(listed(H, N)))
-            nc.scalar.copy(xg1[1][:, :, t], late[:])
+        def gather_late(t, late):
+            nc.vector.tensor_copy(late, x_sb[1, t].indirect(listed(H, N)))
+            nc.scalar.copy(xg1[1][:, :, t], late)
 
-        def quantize_x1(h):
-            xq1 = sb(f"xq1_{h}", [P, H], U32)
+        def quantize_x1(h, xq1):
             xs1 = sb(f"xs1_{h}", [P, H], U8)
-            nc.vector.quantize_mx(out=xq1[:].bitcast(E4M3X4), scales=xs1[:], in_=xg1[h][:].rearrange("p i t -> p (i t)"))
-            score(1, h, xq1[:], xs1[:])
+            nc.vector.quantize_mx(out=xq1.bitcast(E4M3X4), scales=xs1[:], in_=xg1[h][:].rearrange("p i t -> p (i t)"))
+            score(1, h, xq1, xs1[:])
 
         nc.vector.tensor_copy(xg1[0][:, :, 2], x_sb[1, 2].indirect(listed(0, H)))
-        gather_late(2)
+        late2 = sb("late2", [P, H], F32)
+        gather_late(2, late2[:])
         nc.vector.tensor_copy(xg1[0][:, :, 3], x_sb[1, 3].indirect(listed(0, H)))
         deal_wd(1)
-        quantize_x1(0)
-        gather_late(3, tag="wd_raw1")
+        xq1_first = shared.tile([P, H], U32, name="xq1_first", align_bytes=64, offset=0)
+        quantize_x1(0, xq1_first[:])
+        late3 = shared.tile([P, H], F32, name="late3", align_bytes=64, offset=4 * H)
+        gather_late(3, late3[:])
 
         resid = [sb(f"resid{h}", [P, PACK, H], F32) for h in range(HALVES)]
 
@@ -208,7 +214,8 @@ def tile_attend_gml_hub_kernel(tc, xT, wd_words, wd_scales, wv_words, wv_scales,
             nc.vector.quantize_mx(out=gq[:, cols].bitcast(E5M2X4), scales=gs[:, cols], in_=g)
 
         residual(0)
-        quantize_x1(1)
+        xq1_second = sb("xq1_second", [P, H], U32)
+        quantize_x1(1, xq1_second[:])
         clipped = [sb(f"clipped{u}", [P, Q, PACK], F32) for u in range(2)]
         g_first = [sb(f"g{u}", [P, Q * PACK], BF16) for u in range(2)]
         for u in range(2):
@@ -226,13 +233,6 @@ def tile_attend_gml_hub_kernel(tc, xT, wd_words, wd_scales, wv_words, wv_scales,
         residual(1)
         clipped_second = sb("clipped_second", [P, H, PACK], F32)
         clip(clipped_second[:], resid[1][:])
-        g_second = sb("g_second", [P, H * PACK], BF16)
-        nc.gpsimd.tensor_tensor(
-            g_second[:],
-            clipped_second[:].rearrange("p i r -> p (i r)"),
-            c_sb[1][:].rearrange("p i r -> p (i r)"),
-            ALU.mult,
-        )
 
         def back(j, first, bank):
             cols = slice(j * P, (j + 1) * P)
@@ -254,7 +254,15 @@ def tile_attend_gml_hub_kernel(tc, xT, wd_words, wd_scales, wv_words, wv_scales,
             nc.vector.tensor_copy(windows[j % EARLY][:].indirect(listed(lo, hi)), dx[:])
 
         early = [back(j, 0, j) for j in range(EARLY)]
-        for j in range(EARLY - 1):
+        place(0, "dx_early0", early[0][:, H:N], 0, H)
+        g_second = sb("g_second", [P, H * PACK], BF16, tag="dx_early0")
+        nc.gpsimd.tensor_tensor(
+            g_second[:],
+            clipped_second[:].rearrange("p i r -> p (i r)"),
+            c_sb[1][:].rearrange("p i r -> p (i r)"),
+            ALU.mult,
+        )
+        for j in range(1, EARLY - 1):
             place(j, f"dx_early{j}", early[j][:, H:N], 0, H)
         quantize_g(H, N, g_second[:])
         place(EARLY - 1, "dx_early_last", early[EARLY - 1][:, H:N], 0, H, tag="clipped_second")

@@ -78,9 +78,9 @@ def tile_attend_gml_hub_kernel(tc, xT, wd_words, wd_scales, wv_words, wv_scales,
         load_x(0, 0, 2)
         nc.sync.dma_start(offsets[:], offs)
         cw_sb = sb("cw_sb", [P, PACK], F32)
-        nc.sync.dma_start(cw_sb[:], cw.rearrange("(p r) o -> p (r o)", r=PACK))
+        nc.scalar.dma_start(cw_sb[:], cw.rearrange("(p r) o -> p (r o)", r=PACK))
         rw_col = sb("rw_col", [P, PACK], F32)
-        nc.sync.dma_start(rw_col[:], rw[0:1, :].rearrange("o (p j) -> p (o j)", j=PACK))
+        nc.scalar.dma_start(rw_col[:], rw[0:1, :].rearrange("o (p j) -> p (o j)", j=PACK))
         load_x(0, 2, 2)
         load_wd(0)
         for q in range(4):
@@ -198,9 +198,8 @@ def tile_attend_gml_hub_kernel(tc, xT, wd_words, wd_scales, wv_words, wv_scales,
 
         resid = [sb(f"resid{h}", [P, PACK, H], F32) for h in range(HALVES)]
 
-        def residual(h):
-            for r in range(PACK):
-                nc.vector.tensor_tensor(resid[h][:, r, :], a_ps[h][r][:], y_sb[h][:, r, :], ALU.subtract)
+        def residual_part(h, r, lo, hi):
+            nc.vector.tensor_tensor(resid[h][:, r, lo:hi], a_ps[h][r][:, lo:hi], y_sb[h][:, r, lo:hi], ALU.subtract)
 
         def clip(dst, src):
             nc.vector.tensor_scalar(
@@ -213,7 +212,8 @@ def tile_attend_gml_hub_kernel(tc, xT, wd_words, wd_scales, wv_words, wv_scales,
             cols = slice(H + lo, H + hi)
             nc.vector.quantize_mx(out=gq[:, cols].bitcast(E5M2X4), scales=gs[:, cols], in_=g)
 
-        residual(0)
+        for r in range(PACK):
+            residual_part(0, r, 0, H)
         xq1_second = sb("xq1_second", [P, H], U32)
         quantize_x1(1, xq1_second[:])
         clipped = [sb(f"clipped{u}", [P, Q, PACK], F32) for u in range(2)]
@@ -230,9 +230,14 @@ def tile_attend_gml_hub_kernel(tc, xT, wd_words, wd_scales, wv_words, wv_scales,
         for u in range(2):
             quantize_g(u * Q, (u + 1) * Q, g_first[u][:])
 
-        residual(1)
+        for r in range(2):
+            residual_part(1, r, 0, H)
+        for u in range(2):
+            for r in range(2, PACK):
+                residual_part(1, r, u * Q, (u + 1) * Q)
         clipped_second = sb("clipped_second", [P, H, PACK], F32)
-        clip(clipped_second[:], resid[1][:])
+        for u in range(2):
+            clip(clipped_second[:, u * Q : (u + 1) * Q, :], resid[1][:, :, u * Q : (u + 1) * Q])
 
         def back(j, first, bank):
             cols = slice(j * P, (j + 1) * P)

@@ -105,7 +105,7 @@ def tile_attend_gml_hub_kernel(tc, xT, wd_words, wd_scales, wv_words, wv_scales,
                 wv_scales[0, 4 * q : 4 * q + 4, :].bitcast(I32),
             )
 
-        rw_ps = psum.tile([P, PACK, P], F32, name="rw_ps", tag="bank0")
+        rw_ps = psum.tile([P, PACK, P], F32, name="rw_ps", tag="bank7")
         for j in range(PACK):
             nc.tensor.transpose(rw_ps[:, j, :], rw_col[:, j : j + 1].to_broadcast([P, P]), ident[:])
         c_rows = sb("c_rows", [P, PACK, N], F32)
@@ -123,6 +123,22 @@ def tile_attend_gml_hub_kernel(tc, xT, wd_words, wd_scales, wv_words, wv_scales,
                 c_rows[:, :, h * H : (h + 1) * H].rearrange("p r (c i) -> p c r i", i=4),
             )
 
+        c_flat = c_sb[0][:].rearrange("p i r -> p (i r)")
+        turned_ps = psum.tile([P, PACK, P], F32, name="turned_ps", tag="bank7")
+        for j in range(PACK):
+            nc.tensor.transpose(turned_ps[:, j, :], c_flat[:, j * P : (j + 1) * P], ident[:])
+        turned = sb("turned", [P, PACK, P], F32)
+        nc.scalar.copy(turned[:], turned_ps[:])
+        c_ps = psum.tile([P, PACK, P], F32, name="c_ps", tag="bank6")
+        for j in range(PACK):
+            nc.tensor.transpose(c_ps[:, j, :], turned[:, j, :], ident[:])
+        more_turned_ps = psum.tile([P, P], F32, name="more_turned_ps", tag="bank7")
+        nc.tensor.transpose(more_turned_ps[:], c_flat[:, N : N + P], ident[:])
+        more_turned = sb("more_turned", [P, P], F32)
+        nc.scalar.copy(more_turned[:], more_turned_ps[:])
+        more_c_ps = psum.tile([P, P], F32, name="more_c_ps", tag="bank7")
+        nc.tensor.transpose(more_c_ps[:], more_turned[:], ident[:])
+
         wd_sb = [sb(f"wd_sb{o}", [P, V], U32) for o in range(PASSES)]
         wd_sc = sb("wd_sc", [P, V], U8)
 
@@ -133,7 +149,7 @@ def tile_attend_gml_hub_kernel(tc, xT, wd_words, wd_scales, wv_words, wv_scales,
             )
 
         xf0 = sb("xf0", [P, PACK, N], F32)
-        xg0 = sb("xg0", [P, N, PACK], BF16)
+        xg0 = sb("xg0", [P, N, PACK], BF16, tag="c_rows")
         for t in range(PACK):
             nc.vector.tensor_copy(xf0[:, t, :], x_sb[0, t].indirect(offsets[:]))
         deal_wd(0)
@@ -149,23 +165,31 @@ def tile_attend_gml_hub_kernel(tc, xT, wd_words, wd_scales, wv_words, wv_scales,
         xs0 = sb("xs0", [P, N], U8)
         nc.vector.quantize_mx(out=xq0[:].bitcast(E4M3X4), scales=xs0[:], in_=xg0[:].rearrange("p i t -> p (i t)"))
 
-        a_ps = [[psum.tile([P, H], F32, name=f"a{h}_{r}", tag=f"bank{PACK * h + r}") for r in range(PACK)] for h in range(HALVES)]
+        a_first = [psum.tile([P, H], F32, name=f"a_first{r}", tag=f"bank{r}") for r in range(PACK)]
+        a_second = [psum.tile([P, PACK, Q], F32, name=f"a_second{u}", tag=f"bank{PACK + u}") for u in range(2)]
 
-        def score(o, h, codes, scales):
+        def score_pass(o, r, dst, codes, scales, start, stop):
+            cols = slice(r * P, (r + 1) * P)
+            nc.tensor.matmul_mx(
+                out=dst,
+                lhsT=wd_sb[o][:, cols].bitcast(E4M3X4),
+                lhsT_scale=wd_sc[4 * o : P, cols],
+                rhs=codes.bitcast(E4M3X4),
+                rhs_scale=scales,
+                start=start,
+                stop=stop,
+            )
+
+        def score_first(o, codes, scales):
             for r in range(PACK):
-                cols = slice(r * P, (r + 1) * P)
-                nc.tensor.matmul_mx(
-                    out=a_ps[h][r][:],
-                    lhsT=wd_sb[o][:, cols].bitcast(E4M3X4),
-                    lhsT_scale=wd_sc[4 * o : P, cols],
-                    rhs=codes.bitcast(E4M3X4),
-                    rhs_scale=scales,
-                    start=(o == 0),
-                    stop=(o == PASSES - 1),
-                )
+                score_pass(o, r, a_first[r][:], codes, scales, o == 0, o == PASSES - 1)
 
-        for h in range(HALVES):
-            score(0, h, xq0[:, h * H : (h + 1) * H], xs0[:, h * H : (h + 1) * H])
+        def score_second(o, u, codes, scales, opens, closes):
+            for r in range(PACK):
+                score_pass(o, r, a_second[u][:, r, :], codes, scales, opens and r == 0, closes and r == PACK - 1)
+
+        score_first(0, xq0[:, 0:H], xs0[:, 0:H])
+        score_second(0, 0, xq0[:, H : H + Q], xs0[:, H : H + Q], True, False)
 
         xg1 = [sb(f"xg1_{h}", [P, H, PACK], BF16) for h in range(HALVES)]
         xf1 = sb("xf1", [P, 2, N], F32)
@@ -184,7 +208,7 @@ def tile_attend_gml_hub_kernel(tc, xT, wd_words, wd_scales, wv_words, wv_scales,
         def quantize_x1(h, xq1):
             xs1 = sb(f"xs1_{h}", [P, H], U8)
             nc.vector.quantize_mx(out=xq1.bitcast(E4M3X4), scales=xs1[:], in_=xg1[h][:].rearrange("p i t -> p (i t)"))
-            score(1, h, xq1, xs1[:])
+            return xs1
 
         nc.vector.tensor_copy(xg1[0][:, :, 2], x_sb[1, 2].indirect(listed(0, H)))
         late2 = sb("late2", [P, H], F32)
@@ -192,14 +216,9 @@ def tile_attend_gml_hub_kernel(tc, xT, wd_words, wd_scales, wv_words, wv_scales,
         nc.vector.tensor_copy(xg1[0][:, :, 3], x_sb[1, 3].indirect(listed(0, H)))
         deal_wd(1)
         xq1_first = shared.tile([P, H], U32, name="xq1_first", align_bytes=64, offset=0)
-        quantize_x1(0, xq1_first[:])
+        score_first(1, xq1_first[:], quantize_x1(0, xq1_first[:])[:])
         late3 = shared.tile([P, H], F32, name="late3", align_bytes=64, offset=4 * H)
         gather_late(3, late3[:])
-
-        resid = [sb(f"resid{h}", [P, PACK, H], F32) for h in range(HALVES)]
-
-        def residual_part(h, r, lo, hi):
-            nc.vector.tensor_tensor(resid[h][:, r, lo:hi], a_ps[h][r][:, lo:hi], y_sb[h][:, r, lo:hi], ALU.subtract)
 
         def clip(dst, src):
             nc.vector.tensor_scalar(
@@ -212,32 +231,43 @@ def tile_attend_gml_hub_kernel(tc, xT, wd_words, wd_scales, wv_words, wv_scales,
             cols = slice(H + lo, H + hi)
             nc.vector.quantize_mx(out=gq[:, cols].bitcast(E5M2X4), scales=gs[:, cols], in_=g)
 
+        resid_first = sb("resid_first", [P, PACK, H], F32)
         for r in range(PACK):
-            residual_part(0, r, 0, H)
+            nc.vector.tensor_tensor(resid_first[:, r, :], a_first[r][:], y_sb[0][:, r, :], ALU.subtract)
         xq1_second = sb("xq1_second", [P, H], U32)
-        quantize_x1(1, xq1_second[:])
-        clipped = [sb(f"clipped{u}", [P, Q, PACK], F32) for u in range(2)]
-        g_first = [sb(f"g{u}", [P, Q * PACK], BF16) for u in range(2)]
+        xs1_second = quantize_x1(1, xq1_second[:])
+        score_second(1, 0, xq1_second[:, 0:Q], xs1_second[:, 0:Q], False, True)
+        score_second(1, 1, xq1_second[:, Q:H], xs1_second[:, Q:H], True, False)
+        score_second(0, 1, xq0[:, H + Q : N], xs0[:, H + Q : N], False, True)
+        clipped_first = [
+            sb("clipped_quarter0", [P, Q, PACK], F32),
+            shared.tile([P, Q, PACK], F32, name="clipped_quarter1", align_bytes=64, offset=16 * H),
+        ]
         for u in range(2):
-            clip(clipped[u][:], resid[0][:, :, u * Q : (u + 1) * Q])
-        for u in range(2):
-            nc.vector.tensor_tensor(
-                g_first[u][:],
-                clipped[u][:].rearrange("p i r -> p (i r)"),
-                c_sb[0][:, u * Q : (u + 1) * Q, :].rearrange("p i r -> p (i r)"),
-                ALU.mult,
-            )
+            clip(clipped_first[u][:], resid_first[:, :, u * Q : (u + 1) * Q])
+        g_first = [sb(f"g_first{u}", [P, Q * PACK], BF16) for u in range(2)]
+        clipped_flat = [clipped_first[u][:].rearrange("p i r -> p (i r)") for u in range(2)]
+        nc.vector.tensor_tensor(g_first[0][:], clipped_flat[0], c_ps[:].rearrange("p j m -> p (j m)"), ALU.mult)
+        nc.gpsimd.tensor_tensor(g_first[1][:, P:N], clipped_flat[1][:, P:N], c_flat[:, N + P : 2 * N], ALU.mult)
+        nc.vector.tensor_tensor(g_first[1][:, 0:P], clipped_flat[1][:, 0:P], more_c_ps[:], ALU.mult)
+        resid_second = [
+            sb("resid_third", [P, PACK, Q], F32, tag="resid_first"),
+            shared.tile([P, PACK, Q], F32, name="resid_fourth", align_bytes=64, offset=12 * H),
+        ]
+        clipped_second = [
+            shared.tile([P, Q, PACK], F32, name="clipped_third", align_bytes=64, offset=20 * H),
+            sb("clipped_fourth", [P, Q, PACK], F32),
+        ]
+
+        def residual_second(u):
+            nc.vector.tensor_tensor(resid_second[u][:], a_second[u][:], y_sb[1][:, :, u * Q : (u + 1) * Q], ALU.subtract)
+
+        residual_second(0)
         for u in range(2):
             quantize_g(u * Q, (u + 1) * Q, g_first[u][:])
-
-        for r in range(2):
-            residual_part(1, r, 0, H)
+        residual_second(1)
         for u in range(2):
-            for r in range(2, PACK):
-                residual_part(1, r, u * Q, (u + 1) * Q)
-        clipped_second = sb("clipped_second", [P, H, PACK], F32)
-        for u in range(2):
-            clip(clipped_second[:, u * Q : (u + 1) * Q, :], resid[1][:, :, u * Q : (u + 1) * Q])
+            clip(clipped_second[u][:], resid_second[u][:])
 
         def back(j, first, bank):
             cols = slice(j * P, (j + 1) * P)
@@ -261,16 +291,17 @@ def tile_attend_gml_hub_kernel(tc, xT, wd_words, wd_scales, wv_words, wv_scales,
         early = [back(j, 0, j) for j in range(EARLY)]
         place(0, "dx_early0", early[0][:, H:N], 0, H)
         g_second = sb("g_second", [P, H * PACK], BF16, tag="dx_early0")
-        nc.gpsimd.tensor_tensor(
-            g_second[:],
-            clipped_second[:].rearrange("p i r -> p (i r)"),
-            c_sb[1][:].rearrange("p i r -> p (i r)"),
-            ALU.mult,
-        )
+        for u in range(2):
+            nc.gpsimd.tensor_tensor(
+                g_second[:, u * N : (u + 1) * N],
+                clipped_second[u][:].rearrange("p i r -> p (i r)"),
+                c_sb[1][:, u * Q : (u + 1) * Q, :].rearrange("p i r -> p (i r)"),
+                ALU.mult,
+            )
         for j in range(1, EARLY - 1):
             place(j, f"dx_early{j}", early[j][:, H:N], 0, H)
         quantize_g(H, N, g_second[:])
-        place(EARLY - 1, "dx_early_last", early[EARLY - 1][:, H:N], 0, H, tag="clipped_second")
+        place(EARLY - 1, "dx_early_last", early[EARLY - 1][:, H:N], 0, H, tag="clipped_fourth")
         for j in range(D_TILES):
             dx_ps = back(j, H, (j + EARLY) % D_TILES)
             lo = H if j < EARLY else 0

@@ -25,7 +25,8 @@ HALVES = 2
 H = N // HALVES
 Q = H // 2
 D_TILES = D // P
-EARLY = 4
+EARLY = 3
+WINDOWS = 4
 
 
 def tile_attend_gml_hub_kernel(tc, xT, wd_words, wd_scales, wv_words, wv_scales, y, cw, rw, offs, out):
@@ -43,20 +44,20 @@ def tile_attend_gml_hub_kernel(tc, xT, wd_words, wd_scales, wv_words, wv_scales,
         def listed(lo, hi):
             return offsets[:, lo // 16 : hi // 16]
 
-        wd_sc_raw = sb("wd_sc_raw", [P, V], U8)
+        wd_sc_raw = sb("wd_sc_raw", [P, PASSES, V], U8)
         wv_sc = sb("wv_sc", [P, D], U8)
-        nc.gpsimd.memset(wd_sc_raw[:].bitcast(I32), 0)
+        nc.gpsimd.memset(wd_sc_raw[:].rearrange("p o v -> p (o v)").bitcast(I32), 0)
         nc.gpsimd.memset(wv_sc[:].bitcast(I32), 0)
-        gq = sb("gq", [P, H + N], U32)
-        gs = sb("gs", [P, H + N], U8)
-        nc.gpsimd.memset(gq[:, 0:H].bitcast(I32), 0)
-        nc.gpsimd.memset(gs[:, 0:H].bitcast(I32), 0)
+        gq = sb("gq", [P, N], U32)
+        gs = sb("gs", [P, N], U8)
+        nc.gpsimd.memset(gq[:, H:N].bitcast(I32), 0)
+        nc.gpsimd.memset(gs[:, H:N].bitcast(I32), 0)
         ident = sb("ident", [P, P], F32)
         make_identity(nc, ident[:])
-        windows = [sb(f"window{w}", [P, T], F32) for w in range(EARLY)]
-        for w in range(EARLY - 1):
+        windows = [sb(f"window{w}", [P, T], F32) for w in range(WINDOWS)]
+        for w in range(WINDOWS - 1):
             nc.vector.memset(windows[w][:], 0.0)
-        nc.gpsimd.memset(windows[EARLY - 1][:], 0.0)
+        nc.gpsimd.memset(windows[WINDOWS - 1][:], 0.0)
 
         x_planes = xT.rearrange("(o p t) n -> o p t n", o=PASSES, t=PACK)
         x_sb = {}
@@ -85,8 +86,8 @@ def tile_attend_gml_hub_kernel(tc, xT, wd_words, wd_scales, wv_words, wv_scales,
         load_wd(0)
         for q in range(4):
             nc.sync.dma_start(
-                wd_sc_raw[32 * q : 32 * q + 4 * PASSES, :].bitcast(I32),
-                wd_scales[:, 4 * q : 4 * q + 4, :].bitcast(I32),
+                wd_sc_raw[32 * q : 32 * q + 4, :, :].bitcast(I32),
+                wd_scales[:, 4 * q : 4 * q + 4, :].rearrange("o f v -> f o v").bitcast(I32),
             )
         load_x(1, 0, 1)
         load_x(1, 1, 1)
@@ -132,15 +133,17 @@ def tile_attend_gml_hub_kernel(tc, xT, wd_words, wd_scales, wv_words, wv_scales,
         c_ps = psum.tile([P, PACK, P], F32, name="c_ps", tag="bank6")
         for j in range(PACK):
             nc.tensor.transpose(c_ps[:, j, :], turned[:, j, :], ident[:])
-        more_turned_ps = psum.tile([P, P], F32, name="more_turned_ps", tag="bank7")
-        nc.tensor.transpose(more_turned_ps[:], c_flat[:, N : N + P], ident[:])
-        more_turned = sb("more_turned", [P, P], F32)
+        more_turned_ps = psum.tile([P, 2, P], F32, name="more_turned_ps", tag="bank7")
+        for j in range(2):
+            nc.tensor.transpose(more_turned_ps[:, j, :], c_flat[:, N + j * P : N + (j + 1) * P], ident[:])
+        more_turned = sb("more_turned", [P, 2, P], F32)
         nc.scalar.copy(more_turned[:], more_turned_ps[:])
-        more_c_ps = psum.tile([P, P], F32, name="more_c_ps", tag="bank7")
-        nc.tensor.transpose(more_c_ps[:], more_turned[:], ident[:])
+        more_c_ps = psum.tile([P, 2, P], F32, name="more_c_ps", tag="bank7")
+        for j in range(2):
+            nc.tensor.transpose(more_c_ps[:, j, :], more_turned[:, j, :], ident[:])
 
-        wd_sb = [sb(f"wd_sb{o}", [P, V], U32) for o in range(PASSES)]
-        wd_sc = sb("wd_sc", [P, V], U8)
+        wd_sb = [sb("wd_sb0", [P, V], U32, tag="x1_2"), sb("wd_sb1", [P, V], U32)]
+        wd_sc = sb("wd_sc", [P, PASSES, V], U8)
 
         def deal_wd(o):
             nc.vector.tensor_copy(
@@ -152,16 +155,15 @@ def tile_attend_gml_hub_kernel(tc, xT, wd_words, wd_scales, wv_words, wv_scales,
         xg0 = sb("xg0", [P, N, PACK], BF16, tag="c_rows")
         for t in range(PACK):
             nc.vector.tensor_copy(xf0[:, t, :], x_sb[0, t].indirect(offsets[:]))
-        deal_wd(0)
         nc.vector.tensor_copy(
-            wd_sc[:].rearrange("p (r s) -> p s r", r=PACK),
-            wd_sc_raw[:].rearrange("p (s r) -> p s r", r=PACK),
+            wd_sc[:].rearrange("p o (r s) -> p o s r", r=PACK),
+            wd_sc_raw[:].rearrange("p o (s r) -> p o s r", r=PACK),
         )
         nc.scalar.copy(
             xg0[:].rearrange("p (c i) t -> p c t i", i=4),
             xf0[:].rearrange("p t (c i) -> p c t i", i=4),
         )
-        xq0 = sb("xq0", [P, N], U32, tag="x1_1")
+        xq0 = sb("xq0", [P, N], U32)
         xs0 = sb("xs0", [P, N], U8)
         nc.vector.quantize_mx(out=xq0[:].bitcast(E4M3X4), scales=xs0[:], in_=xg0[:].rearrange("p i t -> p (i t)"))
 
@@ -173,7 +175,7 @@ def tile_attend_gml_hub_kernel(tc, xT, wd_words, wd_scales, wv_words, wv_scales,
             nc.tensor.matmul_mx(
                 out=dst,
                 lhsT=wd_sb[o][:, cols].bitcast(E4M3X4),
-                lhsT_scale=wd_sc[4 * o : P, cols],
+                lhsT_scale=wd_sc[:, o, cols],
                 rhs=codes.bitcast(E4M3X4),
                 rhs_scale=scales,
                 start=start,
@@ -188,8 +190,6 @@ def tile_attend_gml_hub_kernel(tc, xT, wd_words, wd_scales, wv_words, wv_scales,
             for r in range(PACK):
                 score_pass(o, r, a_second[u][:, r, :], codes, scales, opens and r == 0, closes and r == PACK - 1)
 
-        score_first(0, xq0[:, 0:H], xs0[:, 0:H])
-        score_second(0, 0, xq0[:, H : H + Q], xs0[:, H : H + Q], True, False)
 
         xg1 = [sb(f"xg1_{h}", [P, H, PACK], BF16) for h in range(HALVES)]
         xf1 = sb("xf1", [P, 2, N], F32)
@@ -213,6 +213,9 @@ def tile_attend_gml_hub_kernel(tc, xT, wd_words, wd_scales, wv_words, wv_scales,
         nc.vector.tensor_copy(xg1[0][:, :, 2], x_sb[1, 2].indirect(listed(0, H)))
         late2 = sb("late2", [P, H], F32)
         gather_late(2, late2[:])
+        deal_wd(0)
+        score_first(0, xq0[:, 0:H], xs0[:, 0:H])
+        score_second(0, 0, xq0[:, H : H + Q], xs0[:, H : H + Q], True, False)
         nc.vector.tensor_copy(xg1[0][:, :, 3], x_sb[1, 3].indirect(listed(0, H)))
         deal_wd(1)
         xq1_first = shared.tile([P, H], U32, name="xq1_first", align_bytes=64, offset=0)
@@ -228,7 +231,7 @@ def tile_attend_gml_hub_kernel(tc, xT, wd_words, wd_scales, wv_words, wv_scales,
             )
 
         def quantize_g(lo, hi, g):
-            cols = slice(H + lo, H + hi)
+            cols = slice(lo, hi)
             nc.vector.quantize_mx(out=gq[:, cols].bitcast(E5M2X4), scales=gs[:, cols], in_=g)
 
         resid_first = sb("resid_first", [P, PACK, H], F32)
@@ -248,36 +251,33 @@ def tile_attend_gml_hub_kernel(tc, xT, wd_words, wd_scales, wv_words, wv_scales,
         g_first = [sb(f"g_first{u}", [P, Q * PACK], BF16) for u in range(2)]
         clipped_flat = [clipped_first[u][:].rearrange("p i r -> p (i r)") for u in range(2)]
         nc.vector.tensor_tensor(g_first[0][:], clipped_flat[0], c_ps[:].rearrange("p j m -> p (j m)"), ALU.mult)
-        nc.gpsimd.tensor_tensor(g_first[1][:, P:N], clipped_flat[1][:, P:N], c_flat[:, N + P : 2 * N], ALU.mult)
-        nc.vector.tensor_tensor(g_first[1][:, 0:P], clipped_flat[1][:, 0:P], more_c_ps[:], ALU.mult)
+        nc.gpsimd.tensor_tensor(g_first[1][:, H:N], clipped_flat[1][:, H:N], c_flat[:, N + H : 2 * N], ALU.mult)
+        nc.vector.tensor_tensor(g_first[1][:, 0:H], clipped_flat[1][:, 0:H], more_c_ps[:].rearrange("p j m -> p (j m)"), ALU.mult)
         resid_second = [
-            sb("resid_third", [P, PACK, Q], F32, tag="resid_first"),
-            shared.tile([P, PACK, Q], F32, name="resid_fourth", align_bytes=64, offset=12 * H),
+            shared.tile([P, PACK, Q], F32, name="resid_third", align_bytes=64, offset=12 * H),
+            shared.tile([P, PACK, Q], F32, name="resid_fourth", align_bytes=64, offset=20 * H),
         ]
-        clipped_second = [
-            shared.tile([P, Q, PACK], F32, name="clipped_third", align_bytes=64, offset=20 * H),
-            sb("clipped_fourth", [P, Q, PACK], F32),
-        ]
+        clipped_second = [sb("clipped_third", [P, Q, PACK], F32), sb("clipped_fourth", [P, Q, PACK], F32)]
 
         def residual_second(u):
             nc.vector.tensor_tensor(resid_second[u][:], a_second[u][:], y_sb[1][:, :, u * Q : (u + 1) * Q], ALU.subtract)
 
-        residual_second(0)
         for u in range(2):
             quantize_g(u * Q, (u + 1) * Q, g_first[u][:])
-        residual_second(1)
+        for u in range(2):
+            residual_second(u)
         for u in range(2):
             clip(clipped_second[u][:], resid_second[u][:])
 
-        def back(j, first, bank):
+        def back(j, name, bank):
             cols = slice(j * P, (j + 1) * P)
-            dx_ps = psum.tile([P, N], F32, name=f"dx_ps{j}_{first}", tag=f"bank{bank}")
+            dx_ps = psum.tile([P, N], F32, name=f"dx_ps{j}_{name}", tag=f"bank{bank}")
             nc.tensor.matmul_mx(
                 out=dx_ps[:],
                 lhsT=wv_sb[:, cols].bitcast(E4M3X4),
                 lhsT_scale=wv_sc[:, cols],
-                rhs=gq[:, first : first + N].bitcast(E5M2X4),
-                rhs_scale=gs[:, first : first + N],
+                rhs=gq[:].bitcast(E5M2X4),
+                rhs_scale=gs[:],
                 start=True,
                 stop=True,
             )
@@ -286,11 +286,9 @@ def tile_attend_gml_hub_kernel(tc, xT, wd_words, wd_scales, wv_words, wv_scales,
         def place(j, name, src, lo, hi, tag=None):
             dx = sb(name, [P, hi - lo], F32, tag)
             nc.scalar.copy(dx[:], src)
-            nc.vector.tensor_copy(windows[j % EARLY][:].indirect(listed(lo, hi)), dx[:])
+            nc.vector.tensor_copy(windows[j % WINDOWS][:].indirect(listed(lo, hi)), dx[:])
 
-        early = [back(j, 0, j) for j in range(EARLY)]
-        place(0, "dx_early0", early[0][:, H:N], 0, H)
-        g_second = sb("g_second", [P, H * PACK], BF16, tag="dx_early0")
+        g_second = sb("g_second", [P, H * PACK], BF16)
         for u in range(2):
             nc.gpsimd.tensor_tensor(
                 g_second[:, u * N : (u + 1) * N],
@@ -298,12 +296,13 @@ def tile_attend_gml_hub_kernel(tc, xT, wd_words, wd_scales, wv_words, wv_scales,
                 c_sb[1][:, u * Q : (u + 1) * Q, :].rearrange("p i r -> p (i r)"),
                 ALU.mult,
             )
-        for j in range(1, EARLY - 1):
-            place(j, f"dx_early{j}", early[j][:, H:N], 0, H)
+        for j in range(EARLY - 1):
+            place(j, f"dx_early{j}", back(j, "early", j)[:, 0:H], 0, H)
+        last_early = back(EARLY - 1, "early", EARLY - 2)
         quantize_g(H, N, g_second[:])
-        place(EARLY - 1, "dx_early_last", early[EARLY - 1][:, H:N], 0, H, tag="clipped_fourth")
+        place(EARLY - 1, "dx_early_last", last_early[:, 0:H], 0, H, tag="clipped_fourth")
         for j in range(D_TILES):
-            dx_ps = back(j, H, (j + EARLY) % D_TILES)
+            dx_ps = back(j, "whole", (j + 2) % D_TILES)
             lo = H if j < EARLY else 0
             place(j, f"dx{j}", dx_ps[:, lo:N], lo, N)
-            nc.sync.dma_start(out[j * P : (j + 1) * P, :], windows[j % EARLY][:])
+            nc.sync.dma_start(out[j * P : (j + 1) * P, :], windows[j % WINDOWS][:])

@@ -286,7 +286,11 @@ def tile_attend_gml_hub_kernel(tc, xT, wd_words, wd_scales, wv_words, wv_scales,
         def place(j, name, src, lo, hi, tag=None):
             dx = sb(name, [P, hi - lo], F32, tag)
             nc.scalar.copy(dx[:], src)
-            nc.vector.tensor_copy(windows[j % WINDOWS][:].indirect(listed(lo, hi)), dx[:])
+            if j % 2 == 1 and j >= EARLY:
+                for b in range(lo, hi, H):
+                    nc.scalar.activation(windows[j % WINDOWS][:].indirect(listed(b, b + H)), dx[:, b - lo : b - lo + H], COPY)
+            else:
+                nc.vector.tensor_copy(windows[j % WINDOWS][:].indirect(listed(lo, hi)), dx[:])
 
         g_second = sb("g_second", [P, H * PACK], BF16)
         for u in range(2):

@@ -21,12 +21,11 @@ P = 128
 PACK = 4
 K_PASS = P * PACK
 PASSES = D // K_PASS
-HALVES = 2
-H = N // HALVES
-Q = H // 2
+H = N // 2
+Q = N // 4
 D_TILES = D // P
-EARLY = 3
-WINDOWS = 4
+WINDOWS = 5
+VECTOR_WINDOWS = 3
 
 
 def tile_attend_gml_hub_kernel(tc, xT, wd_words, wd_scales, wv_words, wv_scales, y, cw, rw, offs, out):
@@ -48,16 +47,13 @@ def tile_attend_gml_hub_kernel(tc, xT, wd_words, wd_scales, wv_words, wv_scales,
         wv_sc = sb("wv_sc", [P, D], U8)
         nc.gpsimd.memset(wd_sc_raw[:].rearrange("p o v -> p (o v)").bitcast(I32), 0)
         nc.gpsimd.memset(wv_sc[:].bitcast(I32), 0)
-        gq = sb("gq", [P, N], U32)
-        gs = sb("gs", [P, N], U8)
-        nc.gpsimd.memset(gq[:, H:N].bitcast(I32), 0)
-        nc.gpsimd.memset(gs[:, H:N].bitcast(I32), 0)
+        zeros = sb("zeros", [P, Q], F32)
+        nc.gpsimd.memset(zeros[:], 0.0)
         ident = sb("ident", [P, P], F32)
         make_identity(nc, ident[:])
         windows = [sb(f"window{w}", [P, T], F32) for w in range(WINDOWS)]
-        for w in range(WINDOWS - 1):
-            nc.vector.memset(windows[w][:], 0.0)
-        nc.gpsimd.memset(windows[WINDOWS - 1][:], 0.0)
+        for w in range(WINDOWS):
+            (nc.vector if w < VECTOR_WINDOWS else nc.gpsimd).memset(windows[w][:], 0.0)
 
         x_planes = xT.rearrange("(o p t) n -> o p t n", o=PASSES, t=PACK)
         x_sb = {}
@@ -89,14 +85,12 @@ def tile_attend_gml_hub_kernel(tc, xT, wd_words, wd_scales, wv_words, wv_scales,
                 wd_sc_raw[32 * q : 32 * q + 4, :, :].bitcast(I32),
                 wd_scales[:, 4 * q : 4 * q + 4, :].rearrange("o f v -> f o v").bitcast(I32),
             )
-        load_x(1, 0, 1)
-        load_x(1, 1, 1)
-        load_x(1, 2, 1)
-        load_x(1, 3, 1)
+        for t in range(PACK):
+            load_x(1, t, 1)
         load_wd(1)
         y_rows = y.rearrange("(p r) i -> p r i", r=PACK)
-        y_sb = [sb(f"y{h}", [P, PACK, H], F32) for h in range(HALVES)]
-        for h in range(HALVES):
+        y_sb = [sb(f"y{h}", [P, PACK, H], F32) for h in range(2)]
+        for h in range(2):
             nc.sync.dma_start(y_sb[h][:], y_rows[:, :, h * H : (h + 1) * H])
         wv_sb = sb("wv_sb", [P, D], U32)
         nc.sync.dma_start(wv_sb[:].bitcast(I32), wv_words[0].rearrange("p n t -> p (n t)").bitcast(I32))
@@ -117,30 +111,11 @@ def tile_attend_gml_hub_kernel(tc, xT, wd_words, wd_scales, wv_words, wv_scales,
                 COPY,
                 scale=cw_sb[:, r : r + 1],
             )
-        c_sb = [sb(f"c{h}", [P, H, PACK], F32) for h in range(HALVES)]
-        for h in range(HALVES):
-            nc.scalar.copy(
-                c_sb[h][:].rearrange("p (c i) r -> p c r i", i=4),
-                c_rows[:, :, h * H : (h + 1) * H].rearrange("p r (c i) -> p c r i", i=4),
-            )
-
-        c_flat = c_sb[0][:].rearrange("p i r -> p (i r)")
-        turned_ps = psum.tile([P, PACK, P], F32, name="turned_ps", tag="bank7")
-        for j in range(PACK):
-            nc.tensor.transpose(turned_ps[:, j, :], c_flat[:, j * P : (j + 1) * P], ident[:])
-        turned = sb("turned", [P, PACK, P], F32)
-        nc.scalar.copy(turned[:], turned_ps[:])
-        c_ps = psum.tile([P, PACK, P], F32, name="c_ps", tag="bank6")
-        for j in range(PACK):
-            nc.tensor.transpose(c_ps[:, j, :], turned[:, j, :], ident[:])
-        more_turned_ps = psum.tile([P, 2, P], F32, name="more_turned_ps", tag="bank7")
-        for j in range(2):
-            nc.tensor.transpose(more_turned_ps[:, j, :], c_flat[:, N + j * P : N + (j + 1) * P], ident[:])
-        more_turned = sb("more_turned", [P, 2, P], F32)
-        nc.scalar.copy(more_turned[:], more_turned_ps[:])
-        more_c_ps = psum.tile([P, 2, P], F32, name="more_c_ps", tag="bank7")
-        for j in range(2):
-            nc.tensor.transpose(more_c_ps[:, j, :], more_turned[:, j, :], ident[:])
+        c_sb = sb("c_sb", [P, N, PACK], F32)
+        nc.scalar.copy(
+            c_sb[:].rearrange("p (c i) r -> p c r i", i=4),
+            c_rows[:].rearrange("p r (c i) -> p c r i", i=4),
+        )
 
         wd_sb = [sb("wd_sb0", [P, V], U32, tag="x1_2"), sb("wd_sb1", [P, V], U32)]
         wd_sc = sb("wd_sc", [P, PASSES, V], U8)
@@ -151,6 +126,17 @@ def tile_attend_gml_hub_kernel(tc, xT, wd_words, wd_scales, wv_words, wv_scales,
                 wd_raw[o][:].bitcast(I32).rearrange("p (s r) -> p s r", r=PACK),
             )
 
+        def weave(dst, src):
+            nc.scalar.copy(
+                dst.rearrange("p (c i) t -> p c t i", i=4),
+                src.rearrange("p t (c i) -> p c t i", i=4),
+            )
+
+        def quantize_x(codes, name, woven):
+            scales = sb(name, [P, codes.shape[1]], U8)
+            nc.vector.quantize_mx(out=codes.bitcast(E4M3X4), scales=scales[:], in_=woven.rearrange("p i t -> p (i t)"))
+            return scales
+
         xf0 = sb("xf0", [P, PACK, N], F32)
         xg0 = sb("xg0", [P, N, PACK], BF16, tag="c_rows")
         for t in range(PACK):
@@ -159,154 +145,141 @@ def tile_attend_gml_hub_kernel(tc, xT, wd_words, wd_scales, wv_words, wv_scales,
             wd_sc[:].rearrange("p o (r s) -> p o s r", r=PACK),
             wd_sc_raw[:].rearrange("p o (s r) -> p o s r", r=PACK),
         )
-        nc.scalar.copy(
-            xg0[:].rearrange("p (c i) t -> p c t i", i=4),
-            xf0[:].rearrange("p t (c i) -> p c t i", i=4),
-        )
+        weave(xg0[:], xf0[:])
         xq0 = sb("xq0", [P, N], U32)
-        xs0 = sb("xs0", [P, N], U8)
-        nc.vector.quantize_mx(out=xq0[:].bitcast(E4M3X4), scales=xs0[:], in_=xg0[:].rearrange("p i t -> p (i t)"))
+        xs0 = quantize_x(xq0[:], "xs0", xg0[:])
 
-        a_first = [psum.tile([P, H], F32, name=f"a_first{r}", tag=f"bank{r}") for r in range(PACK)]
-        a_second = [psum.tile([P, PACK, Q], F32, name=f"a_second{u}", tag=f"bank{PACK + u}") for u in range(2)]
+        scores = [psum.tile([P, PACK, Q], F32, name=f"scores{u}", tag=f"bank{u}") for u in range(4)]
 
-        def score_pass(o, r, dst, codes, scales, start, stop):
-            cols = slice(r * P, (r + 1) * P)
-            nc.tensor.matmul_mx(
-                out=dst,
-                lhsT=wd_sb[o][:, cols].bitcast(E4M3X4),
-                lhsT_scale=wd_sc[:, o, cols],
-                rhs=codes.bitcast(E4M3X4),
-                rhs_scale=scales,
-                start=start,
-                stop=stop,
-            )
-
-        def score_first(o, codes, scales):
+        def score(o, u, codes, scales):
             for r in range(PACK):
-                score_pass(o, r, a_first[r][:], codes, scales, o == 0, o == PASSES - 1)
+                cols = slice(r * P, (r + 1) * P)
+                nc.tensor.matmul_mx(
+                    out=scores[u][:, r, :],
+                    lhsT=wd_sb[o][:, cols].bitcast(E4M3X4),
+                    lhsT_scale=wd_sc[:, o, cols],
+                    rhs=codes.bitcast(E4M3X4),
+                    rhs_scale=scales,
+                    start=(o == 0 and r == 0),
+                    stop=(o == PASSES - 1 and r == PACK - 1),
+                )
 
-        def score_second(o, u, codes, scales, opens, closes):
-            for r in range(PACK):
-                score_pass(o, r, a_second[u][:, r, :], codes, scales, opens and r == 0, closes and r == PACK - 1)
-
-
-        xg1 = [sb(f"xg1_{h}", [P, H, PACK], BF16) for h in range(HALVES)]
-        xf1 = sb("xf1", [P, 2, N], F32)
+        xg1 = [sb(f"xg1_{h}", [P, H, PACK], BF16) for h in range(2)]
+        xf1_first = sb("xf1_first", [P, 2, H], F32)
+        xf1_second = sb("xf1_second", [P, PACK, H], F32)
         for t in range(2):
-            nc.vector.tensor_copy(xf1[:, t, :], x_sb[1, t].indirect(offsets[:]))
-        for h in range(HALVES):
-            nc.scalar.copy(
-                xg1[h][:, :, 0:2].rearrange("p (c i) t -> p c t i", i=4),
-                xf1[:, :, h * H : (h + 1) * H].rearrange("p t (c i) -> p c t i", i=4),
-            )
-
-        def gather_late(t, late):
-            nc.vector.tensor_copy(late, x_sb[1, t].indirect(listed(H, N)))
-            nc.scalar.copy(xg1[1][:, :, t], late)
-
-        def quantize_x1(h, xq1):
-            xs1 = sb(f"xs1_{h}", [P, H], U8)
-            nc.vector.quantize_mx(out=xq1.bitcast(E4M3X4), scales=xs1[:], in_=xg1[h][:].rearrange("p i t -> p (i t)"))
-            return xs1
-
+            nc.vector.tensor_copy(xf1_first[:, t, :], x_sb[1, t].indirect(listed(0, H)))
+            nc.vector.tensor_copy(xf1_second[:, t, :], x_sb[1, t].indirect(listed(H, N)))
+        weave(xg1[0][:, :, 0:2], xf1_first[:])
         nc.vector.tensor_copy(xg1[0][:, :, 2], x_sb[1, 2].indirect(listed(0, H)))
-        late2 = sb("late2", [P, H], F32)
-        gather_late(2, late2[:])
+        nc.scalar.activation(xf1_second[:, 2, :], x_sb[1, 2].indirect(listed(H, N)), COPY)
         deal_wd(0)
-        score_first(0, xq0[:, 0:H], xs0[:, 0:H])
-        score_second(0, 0, xq0[:, H : H + Q], xs0[:, H : H + Q], True, False)
+        for u in range(4):
+            score(0, u, xq0[:, u * Q : (u + 1) * Q], xs0[:, u * Q : (u + 1) * Q])
         nc.vector.tensor_copy(xg1[0][:, :, 3], x_sb[1, 3].indirect(listed(0, H)))
+        nc.scalar.activation(xf1_second[:, 3, :], x_sb[1, 3].indirect(listed(H, N)), COPY)
         deal_wd(1)
-        xq1_first = shared.tile([P, H], U32, name="xq1_first", align_bytes=64, offset=0)
-        score_first(1, xq1_first[:], quantize_x1(0, xq1_first[:])[:])
-        late3 = shared.tile([P, H], F32, name="late3", align_bytes=64, offset=4 * H)
-        gather_late(3, late3[:])
+        xq1 = [
+            shared.tile([P, H], U32, name="xq1_first", align_bytes=64, offset=0),
+            sb("xq1_second", [P, H], U32),
+        ]
 
-        def clip(dst, src):
+        def score_half(h):
+            xs1 = quantize_x(xq1[h][:], f"xs1_{h}", xg1[h][:])
+            for e in range(2):
+                score(1, 2 * h + e, xq1[h][:, e * Q : (e + 1) * Q], xs1[:, e * Q : (e + 1) * Q])
+
+        resid = [sb(f"resid{u}", [P, PACK, Q], F32) for u in range(4)]
+        clipped = [sb(f"clipped{u}", [P, Q, PACK], F32) for u in range(4)]
+        g = [sb(f"g{h}", [P, H * PACK], BF16) for h in range(2)]
+        gq = [sb(f"gq{h}", [P, H], U32) for h in range(2)]
+        gs = [sb(f"gs{h}", [P, H], U8) for h in range(2)]
+
+        def residual(u):
+            nc.vector.tensor_tensor(resid[u][:], scores[u][:], y_sb[u // 2][:, :, (u % 2) * Q : (u % 2 + 1) * Q], ALU.subtract)
+
+        def clip(u):
             nc.vector.tensor_scalar(
-                dst.rearrange("p (c i) r -> p c r i", i=4),
-                src.rearrange("p r (c i) -> p c r i", i=4),
+                clipped[u][:].rearrange("p (c i) r -> p c r i", i=4),
+                resid[u][:].rearrange("p r (c i) -> p c r i", i=4),
                 -1.0, 1.0, ALU.max, ALU.min,
             )
 
-        def quantize_g(lo, hi, g):
-            cols = slice(lo, hi)
-            nc.vector.quantize_mx(out=gq[:, cols].bitcast(E5M2X4), scales=gs[:, cols], in_=g)
+        def weigh(u):
+            nc.vector.tensor_tensor(
+                g[u // 2][:, (u % 2) * N : (u % 2 + 1) * N],
+                clipped[u][:].rearrange("p i r -> p (i r)"),
+                c_sb[:, u * Q : (u + 1) * Q, :].rearrange("p i r -> p (i r)"),
+                ALU.mult,
+            )
 
-        resid_first = sb("resid_first", [P, PACK, H], F32)
-        for r in range(PACK):
-            nc.vector.tensor_tensor(resid_first[:, r, :], a_first[r][:], y_sb[0][:, r, :], ALU.subtract)
-        xq1_second = sb("xq1_second", [P, H], U32)
-        xs1_second = quantize_x1(1, xq1_second[:])
-        score_second(1, 0, xq1_second[:, 0:Q], xs1_second[:, 0:Q], False, True)
-        score_second(1, 1, xq1_second[:, Q:H], xs1_second[:, Q:H], True, False)
-        score_second(0, 1, xq0[:, H + Q : N], xs0[:, H + Q : N], False, True)
-        clipped_first = [
-            sb("clipped_quarter0", [P, Q, PACK], F32),
-            shared.tile([P, Q, PACK], F32, name="clipped_quarter1", align_bytes=64, offset=16 * H),
-        ]
-        for u in range(2):
-            clip(clipped_first[u][:], resid_first[:, :, u * Q : (u + 1) * Q])
-        g_first = [sb(f"g_first{u}", [P, Q * PACK], BF16) for u in range(2)]
-        clipped_flat = [clipped_first[u][:].rearrange("p i r -> p (i r)") for u in range(2)]
-        nc.vector.tensor_tensor(g_first[0][:], clipped_flat[0], c_ps[:].rearrange("p j m -> p (j m)"), ALU.mult)
-        nc.gpsimd.tensor_tensor(g_first[1][:, H:N], clipped_flat[1][:, H:N], c_flat[:, N + H : 2 * N], ALU.mult)
-        nc.vector.tensor_tensor(g_first[1][:, 0:H], clipped_flat[1][:, 0:H], more_c_ps[:].rearrange("p j m -> p (j m)"), ALU.mult)
-        resid_second = [
-            shared.tile([P, PACK, Q], F32, name="resid_third", align_bytes=64, offset=12 * H),
-            shared.tile([P, PACK, Q], F32, name="resid_fourth", align_bytes=64, offset=20 * H),
-        ]
-        clipped_second = [sb("clipped_third", [P, Q, PACK], F32), sb("clipped_fourth", [P, Q, PACK], F32)]
+        def quantize_g(h, lo, hi):
+            nc.vector.quantize_mx(out=gq[h][:, lo:hi].bitcast(E5M2X4), scales=gs[h][:, lo:hi], in_=g[h][:, lo * PACK : hi * PACK])
 
-        def residual_second(u):
-            nc.vector.tensor_tensor(resid_second[u][:], a_second[u][:], y_sb[1][:, :, u * Q : (u + 1) * Q], ALU.subtract)
-
-        for u in range(2):
-            quantize_g(u * Q, (u + 1) * Q, g_first[u][:])
-        for u in range(2):
-            residual_second(u)
-        for u in range(2):
-            clip(clipped_second[u][:], resid_second[u][:])
-
-        def back(j, name, bank):
+        def back_pass(h, j, dst, lo=0, hi=H):
             cols = slice(j * P, (j + 1) * P)
-            dx_ps = psum.tile([P, N], F32, name=f"dx_ps{j}_{name}", tag=f"bank{bank}")
             nc.tensor.matmul_mx(
-                out=dx_ps[:],
+                out=dst,
                 lhsT=wv_sb[:, cols].bitcast(E4M3X4),
                 lhsT_scale=wv_sc[:, cols],
-                rhs=gq[:].bitcast(E5M2X4),
-                rhs_scale=gs[:],
+                rhs=gq[h][:, lo:hi].bitcast(E5M2X4),
+                rhs_scale=gs[h][:, lo:hi],
                 start=True,
                 stop=True,
             )
-            return dx_ps
 
-        def place(j, name, src, lo, hi, tag=None):
-            dx = sb(name, [P, hi - lo], F32, tag)
-            nc.scalar.copy(dx[:], src)
-            if j % 2 == 1 and j >= EARLY:
-                for b in range(lo, hi, H):
-                    nc.scalar.activation(windows[j % WINDOWS][:].indirect(listed(b, b + H)), dx[:, b - lo : b - lo + H], COPY)
-            else:
-                nc.vector.tensor_copy(windows[j % WINDOWS][:].indirect(listed(lo, hi)), dx[:])
+        dx = [{j: sb(f"dx{h}_{j}", [P, H], F32) for j in range(h, D_TILES)} for h in range(2)]
 
-        g_second = sb("g_second", [P, H * PACK], BF16)
-        for u in range(2):
-            nc.gpsimd.tensor_tensor(
-                g_second[:, u * N : (u + 1) * N],
-                clipped_second[u][:].rearrange("p i r -> p (i r)"),
-                c_sb[1][:, u * Q : (u + 1) * Q, :].rearrange("p i r -> p (i r)"),
-                ALU.mult,
-            )
-        for j in range(EARLY - 1):
-            place(j, f"dx_early{j}", back(j, "early", j)[:, 0:H], 0, H)
-        last_early = back(EARLY - 1, "early", EARLY - 2)
-        quantize_g(H, N, g_second[:])
-        place(EARLY - 1, "dx_early_last", last_early[:, 0:H], 0, H, tag="clipped_fourth")
-        for j in range(D_TILES):
-            dx_ps = back(j, "whole", (j + 2) % D_TILES)
-            lo = H if j < EARLY else 0
-            place(j, f"dx{j}", dx_ps[:, lo:N], lo, N)
-            nc.sync.dma_start(out[j * P : (j + 1) * P, :], windows[j % WINDOWS][:])
+        score_half(0)
+        weave(xg1[1][:], xf1_second[:])
+        residual(0)
+        residual(1)
+        score_half(1)
+        clip(0)
+        clip(1)
+        weigh(0)
+        weigh(1)
+        residual(2)
+        quantize_g(0, 0, H)
+        first_banks = [psum.tile([P, 2, H], F32, name=f"dx_first{b}", tag=f"bank{4 + b}") for b in range(4)]
+        back_pass(0, 0, first_banks[0][:, 0, :])
+        nc.scalar.copy(dx[0][0][:], first_banks[0][:, 0, :])
+        for j in range(1, D_TILES):
+            back_pass(0, j, first_banks[j // 2][:, j % 2, :])
+        nc.scalar.activation(windows[0][:].indirect(listed(0, H)), dx[0][0][:], COPY)
+        clip(2)
+        residual(3)
+        weigh(2)
+        clip(3)
+        quantize_g(1, 0, Q)
+        third_ps = psum.tile([P, Q], F32, name="third_ps", tag="bank0")
+        back_pass(1, 0, third_ps[:], 0, Q)
+        weigh(3)
+        third = sb("third", [P, Q], F32)
+        nc.vector.tensor_copy(third[:], third_ps[:])
+        quantize_g(1, Q, H)
+        fourth_ps = psum.tile([P, Q], F32, name="fourth_ps", tag="bank1")
+        back_pass(1, 0, fourth_ps[:], Q, H)
+        second_tags = ["bank2", "bank3", "bank0", "bank1"]
+        second_ps = {}
+        for j in range(1, D_TILES):
+            if j % 2 == 1:
+                bank = psum.tile([P, 2, H], F32, name=f"dx_second{j}", tag=second_tags[j // 2])
+            second_ps[j] = bank[:, (j + 1) % 2, :]
+        back_pass(1, 1, second_ps[1])
+        nc.vector.tensor_tensor(windows[0][:].indirect(listed(H, H + Q)), third[:], zeros[:], ALU.add)
+        fourth = sb("fourth", [P, Q], F32)
+        nc.vector.tensor_copy(fourth[:], fourth_ps[:])
+        nc.vector.tensor_copy(dx[1][1][:], second_ps[1])
+        nc.vector.tensor_tensor(windows[0][:].indirect(listed(H + Q, N)), fourth[:], zeros[:], ALU.add)
+        nc.sync.dma_start(out[0:P, :], windows[0][:])
+        for j in range(2, D_TILES):
+            back_pass(1, j, second_ps[j])
+        for j in range(1, D_TILES):
+            window = windows[j % WINDOWS]
+            nc.scalar.copy(dx[0][j][:], first_banks[j // 2][:, j % 2, :])
+            nc.scalar.activation(window[:].indirect(listed(0, H)), dx[0][j][:], COPY)
+            if j + 1 < D_TILES:
+                nc.vector.tensor_copy(dx[1][j + 1][:], second_ps[j + 1])
+            nc.vector.tensor_copy(window[:].indirect(listed(H, N)), dx[1][j][:])
+            nc.sync.dma_start(out[j * P : (j + 1) * P, :], window[:])

@@ -103,21 +103,29 @@ def tile_attend_gml_hub_kernel(tc, xT, wd_words, wd_scales, wv_words, wv_scales,
         rw_ps = psum.tile([P, PACK, P], F32, name="rw_ps", tag="bank7")
         for j in range(PACK):
             nc.tensor.transpose(rw_ps[:, j, :], rw_col[:, j : j + 1].to_broadcast([P, P]), ident[:])
-        c_rows = sb("c_rows", [P, PACK, N], F32)
-        for r in range(PACK):
-            nc.scalar.activation(
-                c_rows[:, r, :].rearrange("p (s j) -> p s j", j=PACK),
-                rw_ps[:].rearrange("p j s -> p s j"),
-                COPY,
-                scale=cw_sb[:, r : r + 1],
-            )
         c_sb = sb("c_sb", [P, N, PACK], F32)
-        nc.scalar.copy(
-            c_sb[:].rearrange("p (c i) r -> p c r i", i=4),
-            c_rows[:].rearrange("p r (c i) -> p c r i", i=4),
+        nc.vector.tensor_tensor(
+            c_sb[:].rearrange("p (s j) r -> p s j r", j=PACK),
+            rw_ps[:].rearrange("p j s -> p s j").unsqueeze(3).to_broadcast([P, P, PACK, PACK]),
+            cw_sb[:].unsqueeze(1).unsqueeze(1).to_broadcast([P, P, PACK, PACK]),
+            ALU.mult,
         )
 
-        wd_sb = [sb("wd_sb0", [P, V], U32, tag="x1_2"), sb("wd_sb1", [P, V], U32)]
+        c_flat = c_sb[:].rearrange("p i r -> p (i r)")
+
+        def weights_to_psum(name, blocks, via, bank):
+            turned_ps = psum.tile([P, len(blocks), P], F32, name=f"{name}_turned_ps", tag=via)
+            for e, b in enumerate(blocks):
+                nc.tensor.transpose(turned_ps[:, e, :], c_flat[:, b * P : (b + 1) * P], ident[:])
+            turned = sb(f"{name}_turned", [P, len(blocks), P], F32)
+            nc.scalar.copy(turned[:], turned_ps[:])
+            c_ps = psum.tile([P, len(blocks), P], F32, name=name, tag=bank)
+            for e in range(len(blocks)):
+                nc.tensor.transpose(c_ps[:, e, :], turned[:, e, :], ident[:])
+            return c_ps[:].rearrange("p e m -> p (e m)")
+
+
+        wd_sb = [sb("wd_sb0", [P, V], U32), sb("wd_sb1", [P, V], U32)]
         wd_sc = sb("wd_sc", [P, PASSES, V], U8)
 
         def deal_wd(o):
@@ -138,16 +146,17 @@ def tile_attend_gml_hub_kernel(tc, xT, wd_words, wd_scales, wv_words, wv_scales,
             return scales
 
         xf0 = sb("xf0", [P, PACK, N], F32)
-        xg0 = sb("xg0", [P, N, PACK], BF16, tag="c_rows")
-        for t in range(PACK):
+        xg0 = sb("xg0", [P, N, PACK], BF16)
+        for t in range(PACK - 1):
             nc.vector.tensor_copy(xf0[:, t, :], x_sb[0, t].indirect(offsets[:]))
+        for h in range(2):
+            nc.scalar.activation(xf0[:, PACK - 1, h * H : (h + 1) * H], x_sb[0, PACK - 1].indirect(listed(h * H, (h + 1) * H)), COPY)
+            weave(xg0[:, h * H : (h + 1) * H, :], xf0[:, :, h * H : (h + 1) * H])
         nc.vector.tensor_copy(
             wd_sc[:].rearrange("p o (r s) -> p o s r", r=PACK),
             wd_sc_raw[:].rearrange("p o (s r) -> p o s r", r=PACK),
         )
-        weave(xg0[:], xf0[:])
-        xq0 = sb("xq0", [P, N], U32)
-        xs0 = quantize_x(xq0[:], "xs0", xg0[:])
+        deal_wd(0)
 
         scores = [psum.tile([P, PACK, Q], F32, name=f"scores{u}", tag=f"bank{u}") for u in range(4)]
 
@@ -164,30 +173,36 @@ def tile_attend_gml_hub_kernel(tc, xT, wd_words, wd_scales, wv_words, wv_scales,
                     stop=(o == PASSES - 1 and r == PACK - 1),
                 )
 
+        def score_half(o, h, codes):
+            scales = quantize_x(codes[:], f"xs{o}_{h}", xg0[:, h * H : (h + 1) * H, :] if o == 0 else xg1[h][:])
+            for e in range(2):
+                score(o, 2 * h + e, codes[:, e * Q : (e + 1) * Q], scales[:, e * Q : (e + 1) * Q])
+
+        score_half(0, 0, sb("xq0_first", [P, H], U32))
+
+        c_first = weights_to_psum("c_first", [0, 1, 2, 3], "bank6", "bank4")
+        c_more = weights_to_psum("c_more", [4, 8, 9], "bank7", "bank5")
+
         xg1 = [sb(f"xg1_{h}", [P, H, PACK], BF16) for h in range(2)]
-        xf1_first = sb("xf1_first", [P, 2, H], F32)
-        xf1_second = sb("xf1_second", [P, PACK, H], F32)
         for t in range(2):
-            nc.vector.tensor_copy(xf1_first[:, t, :], x_sb[1, t].indirect(listed(0, H)))
-            nc.vector.tensor_copy(xf1_second[:, t, :], x_sb[1, t].indirect(listed(H, N)))
-        weave(xg1[0][:, :, 0:2], xf1_first[:])
+            for h in range(2):
+                nc.vector.tensor_copy(xg1[h][:, :, t], x_sb[1, t].indirect(listed(h * H, (h + 1) * H)))
+
+        def gather_late(t):
+            late = sb(f"late{t}", [P, H], F32)
+            nc.scalar.activation(late[:], x_sb[1, t].indirect(listed(H, N)), COPY)
+            nc.scalar.copy(xg1[1][:, :, t], late[:])
+
         nc.vector.tensor_copy(xg1[0][:, :, 2], x_sb[1, 2].indirect(listed(0, H)))
-        nc.scalar.activation(xf1_second[:, 2, :], x_sb[1, 2].indirect(listed(H, N)), COPY)
-        deal_wd(0)
-        for u in range(4):
-            score(0, u, xq0[:, u * Q : (u + 1) * Q], xs0[:, u * Q : (u + 1) * Q])
+        gather_late(2)
+        score_half(0, 1, sb("xq0_second", [P, H], U32, tag="x1_2"))
         nc.vector.tensor_copy(xg1[0][:, :, 3], x_sb[1, 3].indirect(listed(0, H)))
-        nc.scalar.activation(xf1_second[:, 3, :], x_sb[1, 3].indirect(listed(H, N)), COPY)
+        gather_late(3)
         deal_wd(1)
         xq1 = [
             shared.tile([P, H], U32, name="xq1_first", align_bytes=64, offset=0),
-            sb("xq1_second", [P, H], U32),
+            sb("xq1_second", [P, H], U32, tag="xg1_0"),
         ]
-
-        def score_half(h):
-            xs1 = quantize_x(xq1[h][:], f"xs1_{h}", xg1[h][:])
-            for e in range(2):
-                score(1, 2 * h + e, xq1[h][:, e * Q : (e + 1) * Q], xs1[:, e * Q : (e + 1) * Q])
 
         resid = [sb(f"resid{u}", [P, PACK, Q], F32) for u in range(4)]
         clipped = [sb(f"clipped{u}", [P, Q, PACK], F32) for u in range(4)]
@@ -205,11 +220,11 @@ def tile_attend_gml_hub_kernel(tc, xT, wd_words, wd_scales, wv_words, wv_scales,
                 -1.0, 1.0, ALU.max, ALU.min,
             )
 
-        def weigh(u):
-            nc.vector.tensor_tensor(
-                g[u // 2][:, (u % 2) * N : (u % 2 + 1) * N],
-                clipped[u][:].rearrange("p i r -> p (i r)"),
-                c_sb[:, u * Q : (u + 1) * Q, :].rearrange("p i r -> p (i r)"),
+        def weigh(engine, u, lo, hi, weights=None):
+            engine.tensor_tensor(
+                g[u // 2][:, (u % 2) * N + lo : (u % 2) * N + hi],
+                clipped[u][:].rearrange("p i r -> p (i r)")[:, lo:hi],
+                c_flat[:, u * N + lo : u * N + hi] if weights is None else weights,
                 ALU.mult,
             )
 
@@ -230,37 +245,38 @@ def tile_attend_gml_hub_kernel(tc, xT, wd_words, wd_scales, wv_words, wv_scales,
 
         dx = [{j: sb(f"dx{h}_{j}", [P, H], F32) for j in range(h, D_TILES)} for h in range(2)]
 
-        score_half(0)
-        weave(xg1[1][:], xf1_second[:])
+        score_half(1, 0, xq1[0])
+        score_half(1, 1, xq1[1])
         residual(0)
         residual(1)
-        score_half(1)
         clip(0)
         clip(1)
-        weigh(0)
-        weigh(1)
+        weigh(nc.gpsimd, 1, P, N)
+        weigh(nc.vector, 0, 0, N, c_first)
+        weigh(nc.vector, 1, 0, P, c_more[:, 0:P])
         residual(2)
         quantize_g(0, 0, H)
-        first_banks = [psum.tile([P, 2, H], F32, name=f"dx_first{b}", tag=f"bank{4 + b}") for b in range(4)]
+        first_banks = [psum.tile([P, 2, H], F32, name=f"dx_first{b}", tag=f"bank{(6 + b) % 8}") for b in range(4)]
         back_pass(0, 0, first_banks[0][:, 0, :])
         nc.scalar.copy(dx[0][0][:], first_banks[0][:, 0, :])
         for j in range(1, D_TILES):
             back_pass(0, j, first_banks[j // 2][:, j % 2, :])
         nc.scalar.activation(windows[0][:].indirect(listed(0, H)), dx[0][0][:], COPY)
         clip(2)
+        weigh(nc.gpsimd, 2, H, N)
         residual(3)
-        weigh(2)
+        weigh(nc.vector, 2, 0, H, c_more[:, P : P + H])
         clip(3)
         quantize_g(1, 0, Q)
-        third_ps = psum.tile([P, Q], F32, name="third_ps", tag="bank0")
+        third_ps = psum.tile([P, Q], F32, name="third_ps", tag="bank4")
         back_pass(1, 0, third_ps[:], 0, Q)
-        weigh(3)
+        weigh(nc.vector, 3, 0, N)
         third = sb("third", [P, Q], F32)
         nc.vector.tensor_copy(third[:], third_ps[:])
         quantize_g(1, Q, H)
-        fourth_ps = psum.tile([P, Q], F32, name="fourth_ps", tag="bank1")
+        fourth_ps = psum.tile([P, Q], F32, name="fourth_ps", tag="bank5")
         back_pass(1, 0, fourth_ps[:], Q, H)
-        second_tags = ["bank2", "bank3", "bank0", "bank1"]
+        second_tags = ["bank2", "bank3", "bank4", "bank5"]
         second_ps = {}
         for j in range(1, D_TILES):
             if j % 2 == 1:

@@ -257,10 +257,11 @@ def tile_attend_gml_hub_kernel(tc, xT, wd_words, wd_scales, wv_words, wv_scales,
         residual(2)
         quantize_g(0, 0, H)
         first_banks = [psum.tile([P, 2, H], F32, name=f"dx_first{b}", tag=f"bank{(6 + b) % 8}") for b in range(4)]
-        back_pass(0, 0, first_banks[0][:, 0, :])
-        nc.scalar.copy(dx[0][0][:], first_banks[0][:, 0, :])
+        first_ps = [first_banks[(j + 1) // 2 % 4][:, (j + 1) % 2, :] for j in range(D_TILES)]
+        back_pass(0, 0, first_ps[0])
+        nc.scalar.copy(dx[0][0][:], first_ps[0])
         for j in range(1, D_TILES):
-            back_pass(0, j, first_banks[j // 2][:, j % 2, :])
+            back_pass(0, j, first_ps[j])
         nc.scalar.activation(windows[0][:].indirect(listed(0, H)), dx[0][0][:], COPY)
         clip(2)
         weigh(nc.gpsimd, 2, H, N)
@@ -293,7 +294,7 @@ def tile_attend_gml_hub_kernel(tc, xT, wd_words, wd_scales, wv_words, wv_scales,
             back_pass(1, j, second_ps[j])
         for j in range(1, D_TILES):
             window = windows[j % WINDOWS]
-            nc.scalar.copy(dx[0][j][:], first_banks[j // 2][:, j % 2, :])
+            nc.scalar.copy(dx[0][j][:], first_ps[j])
             nc.scalar.activation(window[:].indirect(listed(0, H)), dx[0][j][:], COPY)
             if j + 1 < D_TILES:
                 nc.vector.tensor_copy(dx[1][j + 1][:], second_ps[j + 1])

@@ -113,8 +113,8 @@ def tile_attend_gml_hub_kernel(tc, xT, wd_words, wd_scales, wv_words, wv_scales,
 
         c_flat = c_sb[:].rearrange("p i r -> p (i r)")
 
-        def weights_to_psum(name, blocks, via, bank):
-            turned_ps = psum.tile([P, len(blocks), P], F32, name=f"{name}_turned_ps", tag=via)
+        def weights_to_psum(name, blocks, bank):
+            turned_ps = psum.tile([P, len(blocks), P], F32, name=f"{name}_turned_ps", tag=bank)
             for e, b in enumerate(blocks):
                 nc.tensor.transpose(turned_ps[:, e, :], c_flat[:, b * P : (b + 1) * P], ident[:])
             turned = sb(f"{name}_turned", [P, len(blocks), P], F32)
@@ -158,7 +158,7 @@ def tile_attend_gml_hub_kernel(tc, xT, wd_words, wd_scales, wv_words, wv_scales,
         )
         deal_wd(0)
 
-        scores = [psum.tile([P, PACK, Q], F32, name=f"scores{u}", tag=f"bank{u}") for u in range(4)]
+        scores = [psum.tile([P, PACK, Q], F32, name=f"scores{u}", tag=f"bank{u if u < 3 else 1}") for u in range(4)]
 
         def score(o, u, codes, scales):
             for r in range(PACK):
@@ -173,15 +173,20 @@ def tile_attend_gml_hub_kernel(tc, xT, wd_words, wd_scales, wv_words, wv_scales,
                     stop=(o == PASSES - 1 and r == PACK - 1),
                 )
 
+        operands = {}
+
         def score_half(o, h, codes):
             scales = quantize_x(codes[:], f"xs{o}_{h}", xg0[:, h * H : (h + 1) * H, :] if o == 0 else xg1[h][:])
             for e in range(2):
-                score(o, 2 * h + e, codes[:, e * Q : (e + 1) * Q], scales[:, e * Q : (e + 1) * Q])
+                operands[o, 2 * h + e] = (codes[:, e * Q : (e + 1) * Q], scales[:, e * Q : (e + 1) * Q])
+                if 2 * h + e < 3:
+                    score(o, 2 * h + e, *operands[o, 2 * h + e])
 
         score_half(0, 0, sb("xq0_first", [P, H], U32))
 
-        c_first = weights_to_psum("c_first", [0, 1, 2, 3], "bank6", "bank4")
-        c_more = weights_to_psum("c_more", [4, 8, 9], "bank7", "bank5")
+        c_first = weights_to_psum("c_first", [0, 1, 2, 3], "bank4")
+        c_more = weights_to_psum("c_more", [4, 8, 9], "bank5")
+        c_fourth = weights_to_psum("c_fourth", [12, 13, 14], "bank3")
 
         xg1 = [sb(f"xg1_{h}", [P, H, PACK], BF16) for h in range(2)]
         for t in range(2):
@@ -249,17 +254,23 @@ def tile_attend_gml_hub_kernel(tc, xT, wd_words, wd_scales, wv_words, wv_scales,
         score_half(1, 1, xq1[1])
         residual(0)
         residual(1)
+        for o in range(PASSES):
+            score(o, 3, *operands[o, 3])
         clip(0)
         clip(1)
         weigh(nc.gpsimd, 1, P, N)
         weigh(nc.vector, 0, 0, N, c_first)
         weigh(nc.vector, 1, 0, P, c_more[:, 0:P])
         residual(2)
-        quantize_g(0, 0, H)
-        first_banks = [psum.tile([P, 2, H], F32, name=f"dx_first{b}", tag=f"bank{(6 + b) % 8}") for b in range(4)]
+        quantize_g(0, 0, Q)
+        quantize_g(0, Q, H)
+        first_banks = [psum.tile([P, 2, H], F32, name=f"dx_first{b}", tag=["bank6", "bank7", "bank0", "bank4"][b]) for b in range(4)]
         first_ps = [first_banks[(j + 1) // 2 % 4][:, (j + 1) % 2, :] for j in range(D_TILES)]
-        back_pass(0, 0, first_ps[0])
-        nc.scalar.copy(dx[0][0][:], first_ps[0])
+        second_quarter_ps = psum.tile([P, Q], F32, name="second_quarter_ps", tag="bank2")
+        back_pass(0, 0, first_ps[0][:, 0:Q], 0, Q)
+        back_pass(0, 0, second_quarter_ps[:], Q, H)
+        nc.scalar.copy(dx[0][0][:, 0:Q], first_ps[0][:, 0:Q])
+        nc.scalar.copy(dx[0][0][:, Q:H], second_quarter_ps[:])
         for j in range(1, D_TILES):
             back_pass(0, j, first_ps[j])
         nc.scalar.activation(windows[0][:].indirect(listed(0, H)), dx[0][0][:], COPY)
@@ -269,15 +280,16 @@ def tile_attend_gml_hub_kernel(tc, xT, wd_words, wd_scales, wv_words, wv_scales,
         weigh(nc.vector, 2, 0, H, c_more[:, P : P + H])
         clip(3)
         quantize_g(1, 0, Q)
-        third_ps = psum.tile([P, Q], F32, name="third_ps", tag="bank4")
+        third_ps = psum.tile([P, Q], F32, name="third_ps", tag="bank5")
         back_pass(1, 0, third_ps[:], 0, Q)
-        weigh(nc.vector, 3, 0, N)
+        weigh(nc.gpsimd, 3, 3 * P, N)
+        weigh(nc.vector, 3, 0, 3 * P, c_fourth)
         third = sb("third", [P, Q], F32)
         nc.vector.tensor_copy(third[:], third_ps[:])
         quantize_g(1, Q, H)
-        fourth_ps = psum.tile([P, Q], F32, name="fourth_ps", tag="bank5")
+        fourth_ps = psum.tile([P, Q], F32, name="fourth_ps", tag="bank1")
         back_pass(1, 0, fourth_ps[:], Q, H)
-        second_tags = ["bank2", "bank3", "bank4", "bank5"]
+        second_tags = ["bank2", "bank3", "bank5", "bank1"]
         second_ps = {}
         for j in range(1, D_TILES):
             if j % 2 == 1:

@@ -26,6 +26,7 @@ Q = N // 4
 D_TILES = D // P
 WINDOWS = 5
 VECTOR_WINDOWS = 3
+THIRD_SHARE = 320
 
 
 def tile_attend_gml_hub_kernel(tc, xT, wd_words, wd_scales, wv_words, wv_scales, y, cw, rw, offs, out):
@@ -185,8 +186,7 @@ def tile_attend_gml_hub_kernel(tc, xT, wd_words, wd_scales, wv_words, wv_scales,
         score_half(0, 0, sb("xq0_first", [P, H], U32))
 
         c_first = weights_to_psum("c_first", [0, 1, 2, 3], "bank4")
-        c_more = weights_to_psum("c_more", [4, 8, 9], "bank5")
-        c_fourth = weights_to_psum("c_fourth", [12, 13, 14], "bank3")
+        c_more = weights_to_psum("c_more", [4, 8, 9, 10], "bank5")
 
         xg1 = [sb(f"xg1_{h}", [P, H, PACK], BF16) for h in range(2)]
         for t in range(2):
@@ -275,15 +275,14 @@ def tile_attend_gml_hub_kernel(tc, xT, wd_words, wd_scales, wv_words, wv_scales,
             back_pass(0, j, first_ps[j])
         nc.scalar.activation(windows[0][:].indirect(listed(0, H)), dx[0][0][:], COPY)
         clip(2)
-        weigh(nc.gpsimd, 2, H, N)
+        weigh(nc.gpsimd, 2, THIRD_SHARE, N)
         residual(3)
-        weigh(nc.vector, 2, 0, H, c_more[:, P : P + H])
+        weigh(nc.vector, 2, 0, THIRD_SHARE, c_more[:, P : P + THIRD_SHARE])
         clip(3)
         quantize_g(1, 0, Q)
         third_ps = psum.tile([P, Q], F32, name="third_ps", tag="bank5")
         back_pass(1, 0, third_ps[:], 0, Q)
-        weigh(nc.gpsimd, 3, 3 * P, N)
-        weigh(nc.vector, 3, 0, 3 * P, c_fourth)
+        weigh(nc.vector, 3, 0, N)
         third = sb("third", [P, Q], F32)
         nc.vector.tensor_copy(third[:], third_ps[:])
         quantize_g(1, Q, H)

@@ -26,6 +26,7 @@ Q = N // 4
 D_TILES = D // P
 WINDOWS = 5
 VECTOR_WINDOWS = 3
+FIRST_SHARE = 64
 THIRD_SHARE = 320
 
 
@@ -177,16 +178,15 @@ def tile_attend_gml_hub_kernel(tc, xT, wd_words, wd_scales, wv_words, wv_scales,
         operands = {}
 
         def score_half(o, h, codes):
-            scales = quantize_x(codes[:], f"xs{o}_{h}", xg0[:, h * H : (h + 1) * H, :] if o == 0 else xg1[h][:])
+            scales = quantize_x(codes[:], f"xs{o}_{h}", xg1[h][:])
             for e in range(2):
                 operands[o, 2 * h + e] = (codes[:, e * Q : (e + 1) * Q], scales[:, e * Q : (e + 1) * Q])
                 if 2 * h + e < 3:
                     score(o, 2 * h + e, *operands[o, 2 * h + e])
 
-        score_half(0, 0, sb("xq0_first", [P, H], U32))
 
-        c_first = weights_to_psum("c_first", [0, 1, 2, 3], "bank4")
-        c_more = weights_to_psum("c_more", [4, 8, 9, 10], "bank5")
+        c_first = weights_to_psum("c_first", [4, 5, 6, 7], "bank4")
+        c_more = weights_to_psum("c_more", [0, 8, 9, 10], "bank5")
 
         xg1 = [sb(f"xg1_{h}", [P, H, PACK], BF16) for h in range(2)]
         for t in range(2):
@@ -200,7 +200,12 @@ def tile_attend_gml_hub_kernel(tc, xT, wd_words, wd_scales, wv_words, wv_scales,
 
         nc.vector.tensor_copy(xg1[0][:, :, 2], x_sb[1, 2].indirect(listed(0, H)))
         gather_late(2)
-        score_half(0, 1, sb("xq0_second", [P, H], U32, tag="x1_2"))
+        xq0 = sb("xq0", [P, N], U32, tag="x1_2")
+        xs0 = quantize_x(xq0[:], "xs0", xg0[:])
+        for u in range(4):
+            operands[0, u] = (xq0[:, u * Q : (u + 1) * Q], xs0[:, u * Q : (u + 1) * Q])
+            if u < 3:
+                score(0, u, *operands[0, u])
         nc.vector.tensor_copy(xg1[0][:, :, 3], x_sb[1, 3].indirect(listed(0, H)))
         gather_late(3)
         deal_wd(1)
@@ -258,19 +263,19 @@ def tile_attend_gml_hub_kernel(tc, xT, wd_words, wd_scales, wv_words, wv_scales,
             score(o, 3, *operands[o, 3])
         clip(0)
         clip(1)
-        weigh(nc.gpsimd, 1, P, N)
-        weigh(nc.vector, 0, 0, N, c_first)
-        weigh(nc.vector, 1, 0, P, c_more[:, 0:P])
+        weigh(nc.gpsimd, 0, FIRST_SHARE, N)
+        weigh(nc.vector, 0, 0, FIRST_SHARE, c_more[:, 0:FIRST_SHARE])
+        weigh(nc.vector, 1, 0, N, c_first)
         residual(2)
-        quantize_g(0, 0, Q)
         quantize_g(0, Q, H)
+        quantize_g(0, 0, Q)
         first_banks = [psum.tile([P, 2, H], F32, name=f"dx_first{b}", tag=["bank6", "bank7", "bank0", "bank4"][b]) for b in range(4)]
         first_ps = [first_banks[(j + 1) // 2 % 4][:, (j + 1) % 2, :] for j in range(D_TILES)]
         second_quarter_ps = psum.tile([P, Q], F32, name="second_quarter_ps", tag="bank2")
-        back_pass(0, 0, first_ps[0][:, 0:Q], 0, Q)
         back_pass(0, 0, second_quarter_ps[:], Q, H)
-        nc.scalar.copy(dx[0][0][:, 0:Q], first_ps[0][:, 0:Q])
+        back_pass(0, 0, first_ps[0][:, 0:Q], 0, Q)
         nc.scalar.copy(dx[0][0][:, Q:H], second_quarter_ps[:])
+        nc.scalar.copy(dx[0][0][:, 0:Q], first_ps[0][:, 0:Q])
         for j in range(1, D_TILES):
             back_pass(0, j, first_ps[j])
         nc.scalar.activation(windows[0][:].indirect(listed(0, H)), dx[0][0][:], COPY)

@@ -28,6 +28,7 @@ WINDOWS = 5
 VECTOR_WINDOWS = 3
 FIRST_SHARE = 64
 THIRD_SHARE = 320
+LAST_SHARE = 384
 
 
 def tile_attend_gml_hub_kernel(tc, xT, wd_words, wd_scales, wv_words, wv_scales, y, cw, rw, offs, out):
@@ -87,7 +88,8 @@ def tile_attend_gml_hub_kernel(tc, xT, wd_words, wd_scales, wv_words, wv_scales,
                 wd_sc_raw[32 * q : 32 * q + 4, :, :].bitcast(I32),
                 wd_scales[:, 4 * q : 4 * q + 4, :].rearrange("o f v -> f o v").bitcast(I32),
             )
-        for t in range(PACK):
+        load_x(1, 0, 2)
+        for t in range(2, PACK):
             load_x(1, t, 1)
         load_wd(1)
         y_rows = y.rearrange("(p r) i -> p r i", r=PACK)
@@ -131,13 +133,19 @@ def tile_attend_gml_hub_kernel(tc, xT, wd_words, wd_scales, wv_words, wv_scales,
         wd_sc = sb("wd_sc", [P, PASSES, V], U8)
 
         def deal_wd(o):
-            nc.vector.tensor_copy(
-                wd_sb[o][:].bitcast(I32).rearrange("p (r s) -> p s r", r=PACK),
-                wd_raw[o][:].bitcast(I32).rearrange("p (s r) -> p s r", r=PACK),
-            )
+            if o == 0:
+                nc.vector.tensor_copy(
+                    wd_sb[o][:].bitcast(I32).rearrange("p (r s) -> p s r", r=PACK),
+                    wd_raw[o][:].bitcast(I32).rearrange("p (s r) -> p s r", r=PACK),
+                )
+            else:
+                nc.scalar.copy(
+                    wd_sb[o][:].rearrange("p (r c i) -> p c r i", r=PACK, i=4),
+                    wd_raw[o][:].rearrange("p (c i r) -> p c r i", r=PACK, i=4),
+                )
 
         def weave(dst, src):
-            nc.scalar.copy(
+            nc.vector.tensor_copy(
                 dst.rearrange("p (c i) t -> p c t i", i=4),
                 src.rearrange("p t (c i) -> p c t i", i=4),
             )
@@ -151,9 +159,8 @@ def tile_attend_gml_hub_kernel(tc, xT, wd_words, wd_scales, wv_words, wv_scales,
         xg0 = sb("xg0", [P, N, PACK], BF16)
         for t in range(PACK - 1):
             nc.vector.tensor_copy(xf0[:, t, :], x_sb[0, t].indirect(offsets[:]))
-        for h in range(2):
-            nc.scalar.activation(xf0[:, PACK - 1, h * H : (h + 1) * H], x_sb[0, PACK - 1].indirect(listed(h * H, (h + 1) * H)), COPY)
-            weave(xg0[:, h * H : (h + 1) * H, :], xf0[:, :, h * H : (h + 1) * H])
+        nc.scalar.activation(xf0[:, PACK - 1, :], x_sb[0, PACK - 1].indirect(offsets[:]), COPY)
+        weave(xg0[:], xf0[:])
         nc.vector.tensor_copy(
             wd_sc[:].rearrange("p o (r s) -> p o s r", r=PACK),
             wd_sc_raw[:].rearrange("p o (s r) -> p o s r", r=PACK),
@@ -187,30 +194,33 @@ def tile_attend_gml_hub_kernel(tc, xT, wd_words, wd_scales, wv_words, wv_scales,
 
         c_first = weights_to_psum("c_first", [4, 5, 6, 7], "bank4")
         c_more = weights_to_psum("c_more", [0, 8, 9, 10], "bank5")
+        c_last = weights_to_psum("c_last", [12, 13, 14], "bank3")
 
         xg1 = [sb(f"xg1_{h}", [P, H, PACK], BF16) for h in range(2)]
+        early = sb("early", [P, 2, H], F32)
         for t in range(2):
-            for h in range(2):
-                nc.vector.tensor_copy(xg1[h][:, :, t], x_sb[1, t].indirect(listed(h * H, (h + 1) * H)))
+            nc.vector.tensor_copy(xg1[0][:, :, t], x_sb[1, t].indirect(listed(0, H)))
+            nc.scalar.activation(early[:, t, :], x_sb[1, t].indirect(listed(H, N)), COPY)
+        weave(xg1[1][:, :, 0:2], early[:])
+
+        late = sb("late", [P, 2, H], F32)
 
         def gather_late(t):
-            late = sb(f"late{t}", [P, H], F32)
-            nc.scalar.activation(late[:], x_sb[1, t].indirect(listed(H, N)), COPY)
-            nc.scalar.copy(xg1[1][:, :, t], late[:])
+            nc.scalar.activation(late[:, t - 2, :], x_sb[1, t].indirect(listed(H, N)), COPY)
 
-        nc.vector.tensor_copy(xg1[0][:, :, 2], x_sb[1, 2].indirect(listed(0, H)))
-        gather_late(2)
-        xq0 = sb("xq0", [P, N], U32, tag="x1_2")
+        xq0 = sb("xq0", [P, N], U32, tag="x1_0")
         xs0 = quantize_x(xq0[:], "xs0", xg0[:])
         for u in range(4):
             operands[0, u] = (xq0[:, u * Q : (u + 1) * Q], xs0[:, u * Q : (u + 1) * Q])
             if u < 3:
                 score(0, u, *operands[0, u])
+        nc.vector.tensor_copy(xg1[0][:, :, 2], x_sb[1, 2].indirect(listed(0, H)))
+        gather_late(2)
         nc.vector.tensor_copy(xg1[0][:, :, 3], x_sb[1, 3].indirect(listed(0, H)))
         gather_late(3)
         deal_wd(1)
         xq1 = [
-            shared.tile([P, H], U32, name="xq1_first", align_bytes=64, offset=0),
+            sb("xq1_first", [P, H], U32),
             sb("xq1_second", [P, H], U32, tag="xg1_0"),
         ]
 
@@ -256,6 +266,7 @@ def tile_attend_gml_hub_kernel(tc, xT, wd_words, wd_scales, wv_words, wv_scales,
         dx = [{j: sb(f"dx{h}_{j}", [P, H], F32) for j in range(h, D_TILES)} for h in range(2)]
 
         score_half(1, 0, xq1[0])
+        weave(xg1[1][:, :, 2:4], late[:])
         score_half(1, 1, xq1[1])
         residual(0)
         residual(1)
@@ -287,7 +298,8 @@ def tile_attend_gml_hub_kernel(tc, xT, wd_words, wd_scales, wv_words, wv_scales,
         quantize_g(1, 0, Q)
         third_ps = psum.tile([P, Q], F32, name="third_ps", tag="bank5")
         back_pass(1, 0, third_ps[:], 0, Q)
-        weigh(nc.vector, 3, 0, N)
+        weigh(nc.vector, 3, 0, LAST_SHARE, c_last)
+        weigh(nc.gpsimd, 3, LAST_SHARE, N)
         third = sb("third", [P, Q], F32)
         nc.vector.tensor_copy(third[:], third_ps[:])
         quantize_g(1, Q, H)

@@ -221,7 +221,7 @@ def tile_attend_gml_hub_kernel(tc, xT, wd_words, wd_scales, wv_words, wv_scales,
         deal_wd(1)
         xq1 = [
             sb("xq1_first", [P, H], U32),
-            sb("xq1_second", [P, H], U32, tag="xg1_0"),
+            sb("xq1_second", [P, H], U32),
         ]
 
         resid = [sb(f"resid{u}", [P, PACK, Q], F32) for u in range(4)]
@@ -265,8 +265,10 @@ def tile_attend_gml_hub_kernel(tc, xT, wd_words, wd_scales, wv_words, wv_scales,
 
         dx = [{j: sb(f"dx{h}_{j}", [P, H], F32) for j in range(h, D_TILES)} for h in range(2)]
 
-        score_half(1, 0, xq1[0])
         weave(xg1[1][:, :, 2:4], late[:])
+        for e in range(2):
+            scales = quantize_x(xq1[0][:, e * Q : (e + 1) * Q], f"xs1_0{e}", xg1[0][:, e * Q : (e + 1) * Q, :])
+            score(1, e, xq1[0][:, e * Q : (e + 1) * Q], scales[:])
         score_half(1, 1, xq1[1])
         residual(0)
         residual(1)

from contextlib import ExitStack

import concourse.mybir as mybir
from concourse.masks import make_identity

N, T, D, V = 512, 2048, 1024, 512
FLOPS = 2 * 2 * N * D * V

F32 = mybir.dt.float32
BF16 = mybir.dt.bfloat16
I32 = mybir.dt.int32
U32 = mybir.dt.uint32
U16 = mybir.dt.uint16
U8 = mybir.dt.uint8
E4M3X4 = mybir.dt.float8_e4m3fn_x4
E5M2X4 = mybir.dt.float8_e5m2_x4
ALU = mybir.AluOpType
COPY = mybir.ActivationFunctionType.Copy

P = 128
PACK = 4
K_PASS = P * PACK
PASSES = D // K_PASS
H = N // 2
Q = N // 4
D_TILES = D // P
WINDOWS = 5
VECTOR_WINDOWS = 3
FIRST_SHARE = 64
THIRD_SHARE = 320
LAST_SHARE = 384


def tile_attend_gml_hub_kernel(tc, xT, wd_words, wd_scales, wv_words, wv_scales, y, cw, rw, offs, out):
    nc = tc.nc
    with ExitStack() as ctx:
        keep = ctx.enter_context(tc.tile_pool(name="keep", bufs=1))
        shared = ctx.enter_context(tc.tile_pool(name="shared", bufs=1))
        psum = ctx.enter_context(tc.psum_pool(name="psum", bufs=1))

        def sb(name, shape, dtype, tag=None):
            return keep.tile(shape, dtype, name=name, tag=tag or name, align_bytes=64)

        offsets = keep.tile([P, N // 16], U16, name="offsets")

        def listed(lo, hi):
            return offsets[:, lo // 16 : hi // 16]

        wd_sc_raw = sb("wd_sc_raw", [P, PASSES, V], U8)
        wv_sc = sb("wv_sc", [P, D], U8)
        nc.gpsimd.memset(wd_sc_raw[:].rearrange("p o v -> p (o v)").bitcast(I32), 0)
        nc.gpsimd.memset(wv_sc[:].bitcast(I32), 0)
        zeros = sb("zeros", [P, Q], F32)
        nc.gpsimd.memset(zeros[:], 0.0)
        ident = sb("ident", [P, P], F32)
        make_identity(nc, ident[:])
        windows = [sb(f"window{w}", [P, T], F32) for w in range(WINDOWS)]
        for w in range(WINDOWS):
            (nc.vector if w < VECTOR_WINDOWS else nc.gpsimd).memset(windows[w][:], 0.0)

        x_planes = xT.rearrange("(o p t) n -> o p t n", o=PASSES, t=PACK)
        x_sb = {}

        def load_x(o, t, count):
            tile = sb(f"x{o}_{t}", [P, count, T], F32)
            nc.sync.dma_start(tile[:], x_planes[o, :, t : t + count, :])
            for e in range(count):
                x_sb[o, t + e] = tile[:, e, :]

        wd_raw = [
            sb("wd_raw0", [P, V], U32),
            shared.tile([P, V], U32, name="wd_raw1", align_bytes=64, offset=0),
        ]

        def load_wd(o):
            nc.sync.dma_start(wd_raw[o][:].bitcast(I32), wd_words[o].rearrange("p n t -> p (n t)").bitcast(I32))

        load_x(0, 0, 2)
        nc.sync.dma_start(offsets[:], offs)
        cw_sb = sb("cw_sb", [P, PACK], F32)
        nc.scalar.dma_start(cw_sb[:], cw.rearrange("(p r) o -> p (r o)", r=PACK))
        rw_col = sb("rw_col", [P, PACK], F32)
        nc.scalar.dma_start(rw_col[:], rw[0:1, :].rearrange("o (p j) -> p (o j)", j=PACK))
        load_x(0, 2, 2)
        load_wd(0)
        for q in range(4):
            nc.sync.dma_start(
                wd_sc_raw[32 * q : 32 * q + 4, :, :].bitcast(I32),
                wd_scales[:, 4 * q : 4 * q + 4, :].rearrange("o f v -> f o v").bitcast(I32),
            )
        load_x(1, 0, 2)
        for t in range(2, PACK):
            load_x(1, t, 1)
        load_wd(1)
        y_rows = y.rearrange("(p r) i -> p r i", r=PACK)
        y_sb = [sb(f"y{h}", [P, PACK, H], F32) for h in range(2)]
        for h in range(2):
            nc.sync.dma_start(y_sb[h][:], y_rows[:, :, h * H : (h + 1) * H])
        wv_sb = sb("wv_sb", [P, D], U32)
        nc.sync.dma_start(wv_sb[:].bitcast(I32), wv_words[0].rearrange("p n t -> p (n t)").bitcast(I32))
        for q in range(4):
            nc.sync.dma_start(
                wv_sc[32 * q : 32 * q + 4, :].bitcast(I32),
                wv_scales[0, 4 * q : 4 * q + 4, :].bitcast(I32),
            )

        rw_ps = psum.tile([P, PACK, P], F32, name="rw_ps", tag="bank7")
        for j in range(PACK):
            nc.tensor.transpose(rw_ps[:, j, :], rw_col[:, j : j + 1].to_broadcast([P, P]), ident[:])
        c_sb = sb("c_sb", [P, N, PACK], F32)
        nc.vector.tensor_tensor(
            c_sb[:].rearrange("p (s j) r -> p s j r", j=PACK),
            rw_ps[:].rearrange("p j s -> p s j").unsqueeze(3).to_broadcast([P, P, PACK, PACK]),
            cw_sb[:].unsqueeze(1).unsqueeze(1).to_broadcast([P, P, PACK, PACK]),
            ALU.mult,
        )

        c_flat = c_sb[:].rearrange("p i r -> p (i r)")

        def weights_to_psum(name, blocks, bank):
            turned_ps = psum.tile([P, len(blocks), P], F32, name=f"{name}_turned_ps", tag=bank)
            for e, b in enumerate(blocks):
                nc.tensor.transpose(turned_ps[:, e, :], c_flat[:, b * P : (b + 1) * P], ident[:])
            turned = sb(f"{name}_turned", [P, len(blocks), P], F32)
            nc.scalar.copy(turned[:], turned_ps[:])
            c_ps = psum.tile([P, len(blocks), P], F32, name=name, tag=bank)
            for e in range(len(blocks)):
                nc.tensor.transpose(c_ps[:, e, :], turned[:, e, :], ident[:])
            return c_ps[:].rearrange("p e m -> p (e m)")


        wd_sb = [sb("wd_sb0", [P, V], U32), sb("wd_sb1", [P, V], U32)]
        wd_sc = sb("wd_sc", [P, PASSES, V], U8)

        def deal_wd(o):
            if o == 0:
                nc.vector.tensor_copy(
                    wd_sb[o][:].bitcast(I32).rearrange("p (r s) -> p s r", r=PACK),
                    wd_raw[o][:].bitcast(I32).rearrange("p (s r) -> p s r", r=PACK),
                )
            else:
                nc.scalar.copy(
                    wd_sb[o][:].rearrange("p (r c i) -> p c r i", r=PACK, i=4),
                    wd_raw[o][:].rearrange("p (c i r) -> p c r i", r=PACK, i=4),
                )

        def weave(dst, src):
            nc.vector.tensor_copy(
                dst.rearrange("p (c i) t -> p c t i", i=4),
                src.rearrange("p t (c i) -> p c t i", i=4),
            )

        def quantize_x(codes, name, woven):
            scales = sb(name, [P, codes.shape[1]], U8)
            nc.vector.quantize_mx(out=codes.bitcast(E4M3X4), scales=scales[:], in_=woven.rearrange("p i t -> p (i t)"))
            return scales

        xf0 = sb("xf0", [P, PACK, N], F32)
        xg0 = sb("xg0", [P, N, PACK], BF16)
        for t in range(PACK - 1):
            nc.vector.tensor_copy(xf0[:, t, :], x_sb[0, t].indirect(offsets[:]))
        nc.scalar.activation(xf0[:, PACK - 1, :], x_sb[0, PACK - 1].indirect(offsets[:]), COPY)
        weave(xg0[:], xf0[:])
        nc.vector.tensor_copy(
            wd_sc[:].rearrange("p o (r s) -> p o s r", r=PACK),
            wd_sc_raw[:].rearrange("p o (s r) -> p o s r", r=PACK),
        )
        deal_wd(0)

        scores = [psum.tile([P, PACK, Q], F32, name=f"scores{u}", tag=f"bank{u if u < 3 else 1}") for u in range(4)]

        def score(o, u, codes, scales):
            for r in range(PACK):
                cols = slice(r * P, (r + 1) * P)
                nc.tensor.matmul_mx(
                    out=scores[u][:, r, :],
                    lhsT=wd_sb[o][:, cols].bitcast(E4M3X4),
                    lhsT_scale=wd_sc[:, o, cols],
                    rhs=codes.bitcast(E4M3X4),
                    rhs_scale=scales,
                    start=(o == 0 and r == 0),
                    stop=(o == PASSES - 1 and r == PACK - 1),
                )

        operands = {}

        def score_half(o, h, codes):
            scales = quantize_x(codes[:], f"xs{o}_{h}", xg1[h][:])
            for e in range(2):
                operands[o, 2 * h + e] = (codes[:, e * Q : (e + 1) * Q], scales[:, e * Q : (e + 1) * Q])
                if 2 * h + e < 3:
                    score(o, 2 * h + e, *operands[o, 2 * h + e])


        c_first = weights_to_psum("c_first", [4, 5, 6, 7], "bank4")
        c_more = weights_to_psum("c_more", [0, 8, 9, 10], "bank5")
        c_last = weights_to_psum("c_last", [12, 13, 14], "bank3")

        xg1 = [sb(f"xg1_{h}", [P, H, PACK], BF16) for h in range(2)]
        early = sb("early", [P, 2, H], F32)
        for t in range(2):
            nc.vector.tensor_copy(xg1[0][:, :, t], x_sb[1, t].indirect(listed(0, H)))
            nc.scalar.activation(early[:, t, :], x_sb[1, t].indirect(listed(H, N)), COPY)
        weave(xg1[1][:, :, 0:2], early[:])

        late = sb("late", [P, 2, H], F32)

        def gather_late(t):
            nc.scalar.activation(late[:, t - 2, :], x_sb[1, t].indirect(listed(H, N)), COPY)

        xq0 = sb("xq0", [P, N], U32, tag="x1_0")
        xs0 = quantize_x(xq0[:], "xs0", xg0[:])
        for u in range(4):
            operands[0, u] = (xq0[:, u * Q : (u + 1) * Q], xs0[:, u * Q : (u + 1) * Q])
            if u < 3:
                score(0, u, *operands[0, u])
        nc.vector.tensor_copy(xg1[0][:, :, 2], x_sb[1, 2].indirect(listed(0, H)))
        gather_late(2)
        nc.vector.tensor_copy(xg1[0][:, :, 3], x_sb[1, 3].indirect(listed(0, H)))
        gather_late(3)
        deal_wd(1)
        xq1 = [
            sb("xq1_first", [P, H], U32),
            sb("xq1_second", [P, H], U32),
        ]

        resid = [sb(f"resid{u}", [P, PACK, Q], F32) for u in range(4)]
        clipped = [sb(f"clipped{u}", [P, Q, PACK], F32) for u in range(4)]
        g = [sb(f"g{h}", [P, H * PACK], BF16) for h in range(2)]
        gq = [sb(f"gq{h}", [P, H], U32) for h in range(2)]
        gs = [sb(f"gs{h}", [P, H], U8) for h in range(2)]

        def residual(u):
            nc.vector.tensor_tensor(resid[u][:], scores[u][:], y_sb[u // 2][:, :, (u % 2) * Q : (u % 2 + 1) * Q], ALU.subtract)

        def clip(u):
            nc.vector.tensor_scalar(
                clipped[u][:].rearrange("p (c i) r -> p c r i", i=4),
                resid[u][:].rearrange("p r (c i) -> p c r i", i=4),
                -1.0, 1.0, ALU.max, ALU.min,
            )

        def weigh(engine, u, lo, hi, weights=None):
            engine.tensor_tensor(
                g[u // 2][:, (u % 2) * N + lo : (u % 2) * N + hi],
                clipped[u][:].rearrange("p i r -> p (i r)")[:, lo:hi],
                c_flat[:, u * N + lo : u * N + hi] if weights is None else weights,
                ALU.mult,
            )

        def quantize_g(h, lo, hi):
            nc.vector.quantize_mx(out=gq[h][:, lo:hi].bitcast(E5M2X4), scales=gs[h][:, lo:hi], in_=g[h][:, lo * PACK : hi * PACK])

        def back_pass(h, j, dst, lo=0, hi=H):
            cols = slice(j * P, (j + 1) * P)
            nc.tensor.matmul_mx(
                out=dst,
                lhsT=wv_sb[:, cols].bitcast(E4M3X4),
                lhsT_scale=wv_sc[:, cols],
                rhs=gq[h][:, lo:hi].bitcast(E5M2X4),
                rhs_scale=gs[h][:, lo:hi],
                start=True,
                stop=True,
            )

        dx = [{j: sb(f"dx{h}_{j}", [P, H], F32) for j in range(h, D_TILES)} for h in range(2)]

        weave(xg1[1][:, :, 2:4], late[:])
        for e in range(2):
            scales = quantize_x(xq1[0][:, e * Q : (e + 1) * Q], f"xs1_0{e}", xg1[0][:, e * Q : (e + 1) * Q, :])
            score(1, e, xq1[0][:, e * Q : (e + 1) * Q], scales[:])
        score_half(1, 1, xq1[1])
        residual(0)
        residual(1)
        for o in range(PASSES):
            score(o, 3, *operands[o, 3])
        clip(0)
        clip(1)
        weigh(nc.gpsimd, 0, FIRST_SHARE, N)
        weigh(nc.vector, 0, 0, FIRST_SHARE, c_more[:, 0:FIRST_SHARE])
        weigh(nc.vector, 1, 0, N, c_first)
        residual(2)
        quantize_g(0, Q, H)
        quantize_g(0, 0, Q)
        first_banks = [psum.tile([P, 2, H], F32, name=f"dx_first{b}", tag=["bank6", "bank7", "bank0", "bank4"][b]) for b in range(4)]
        first_ps = [first_banks[(j + 1) // 2 % 4][:, (j + 1) % 2, :] for j in range(D_TILES)]
        second_quarter_ps = psum.tile([P, Q], F32, name="second_quarter_ps", tag="bank2")
        back_pass(0, 0, second_quarter_ps[:], Q, H)
        back_pass(0, 0, first_ps[0][:, 0:Q], 0, Q)
        nc.scalar.copy(dx[0][0][:, Q:H], second_quarter_ps[:])
        nc.scalar.copy(dx[0][0][:, 0:Q], first_ps[0][:, 0:Q])
        for j in range(1, D_TILES):
            back_pass(0, j, first_ps[j])
        nc.scalar.activation(windows[0][:].indirect(listed(0, H)), dx[0][0][:], COPY)
        clip(2)
        weigh(nc.gpsimd, 2, THIRD_SHARE, N)
        residual(3)
        weigh(nc.vector, 2, 0, THIRD_SHARE, c_more[:, P : P + THIRD_SHARE])
        clip(3)
        quantize_g(1, 0, Q)
        third_ps = psum.tile([P, Q], F32, name="third_ps", tag="bank5")
        back_pass(1, 0, third_ps[:], 0, Q)
        weigh(nc.vector, 3, 0, LAST_SHARE, c_last)
        weigh(nc.gpsimd, 3, LAST_SHARE, N)
        third = sb("third", [P, Q], F32)
        nc.vector.tensor_copy(third[:], third_ps[:])
        quantize_g(1, Q, H)
        fourth_ps = psum.tile([P, Q], F32, name="fourth_ps", tag="bank1")
        back_pass(1, 0, fourth_ps[:], Q, H)
        second_tags = ["bank2", "bank3", "bank5", "bank1"]
        second_ps = {}
        for j in range(1, D_TILES):
            if j % 2 == 1:
                bank = psum.tile([P, 2, H], F32, name=f"dx_second{j}", tag=second_tags[j // 2])
            second_ps[j] = bank[:, (j + 1) % 2, :]
        back_pass(1, 1, second_ps[1])
        nc.vector.tensor_tensor(windows[0][:].indirect(listed(H, H + Q)), third[:], zeros[:], ALU.add)
        fourth = sb("fourth", [P, Q], F32)
        nc.vector.tensor_copy(fourth[:], fourth_ps[:])
        nc.vector.tensor_copy(dx[1][1][:], second_ps[1])
        nc.vector.tensor_tensor(windows[0][:].indirect(listed(H + Q, N)), fourth[:], zeros[:], ALU.add)
        nc.sync.dma_start(out[0:P, :], windows[0][:])
        for j in range(2, D_TILES):
            back_pass(1, j, second_ps[j])
        for j in range(1, D_TILES):
            window = windows[j % WINDOWS]
            nc.scalar.copy(dx[0][j][:], first_ps[j])
            nc.scalar.activation(window[:].indirect(listed(0, H)), dx[0][j][:], COPY)
            if j + 1 < D_TILES:
                nc.vector.tensor_copy(dx[1][j + 1][:], second_ps[j + 1])
            nc.vector.tensor_copy(window[:].indirect(listed(H, N)), dx[1][j][:])
            nc.sync.dma_start(out[j * P : (j + 1) * P, :], window[:])
